import numpy as np
import ml_dtypes


def mxq(x, axis, fmt="e4m3"):
    dtype, down = {"e4m3": (ml_dtypes.float8_e4m3fn, 7), "e5m2": (ml_dtypes.float8_e5m2, 14)}[fmt]
    v = np.moveaxis(np.asarray(x, np.float32).astype(ml_dtypes.bfloat16).astype(np.float64), axis, -1)
    blocks = v.reshape(v.shape[:-1] + (-1, 32))
    amax = np.abs(blocks).max(-1, keepdims=True)
    byte = np.maximum(np.where(amax > 0, np.frexp(amax)[1] - 1 + 127, 0) - down, 1)
    scale = np.exp2(byte - 127.0)
    codes = (blocks / scale).astype(np.float32).astype(dtype).astype(np.float64)
    return np.moveaxis((codes * scale).reshape(v.shape), -1, axis)


WIDE = False


def mx_kscale(k):
    if not WIDE:
        return np.ones(k)
    levels = np.array([10, -10, 5, -5, 0])
    if k % 512:
        return np.exp2(np.random.permutation(np.resize(levels, k // 32))).repeat(32)
    a = np.empty((k // 512, 16))
    for p in range(k // 512):
        a[p, :8] = np.random.permutation(np.resize(levels, 8))
        for g in range(8):
            far = levels[np.abs(levels - a[p, g]) >= 10]
            a[p, g + 8] = far[np.random.randint(len(far))]
    return np.exp2(a.ravel()).repeat(32)


def f64(x):
    return np.asarray(x).astype(np.float64)


def striped(idx):
    return np.tile(idx.reshape(-1, 16).T, (8, 1)).astype(np.uint16)


def unstriped(offs):
    return offs[:16].T.reshape(-1).astype(np.int64)

def planes(y):
    n, m = y.shape
    v = y.astype(np.float32).astype(ml_dtypes.bfloat16).astype(np.float64).reshape(n // 32, 32, m)
    top = np.abs(v).max(1)
    byte = np.clip(np.where(top > 0, np.frexp(top)[1] - 1 + 127 - 7, 1), 1, 254)
    codes = (v * np.exp2(127.0 - byte)[:, None, :]).reshape(n, m).astype(np.float32).astype(ml_dtypes.float8_e4m3fn).view(np.uint8)
    words = codes.reshape(n // 512, 128, 4, m).transpose(0, 1, 3, 2)
    return np.ascontiguousarray(words), np.ascontiguousarray(byte.astype(np.uint8).reshape(n // 512, 16, m))


K, T, S, N = 512, 1024, 512, 512
P = 2 ** 7


def setup_inputs():
    n = np.random.standard_normal
    s = mx_kscale(K)[:, None]
    return {
        "xT": (n((K, T)) * s).astype(np.float32),
        "tscale": np.tile(np.random.uniform(0.25, 2.0, T), (P, 1)).astype(np.float32),
        "cscale": np.random.uniform(0.5, 1.5, (N, 1)).astype(np.float32),
        "w1": (n((K, N)) / np.sqrt(K) / s).astype(np.float32),
        "offs": striped(np.random.permutation(T)[:S]),
    }


def reference(xT, tscale, cscale, w1, offs):
    xq = mxq(f64(xT)[:, unstriped(offs)], 0, "e4m3")
    y = mxq(f64(w1), 0, "e4m3").T @ xq
    tg = f64(tscale)[:1][:, unstriped(offs)]
    out_0 = (f64(cscale) * y) * tg
    return (out_0,) + planes(out_0)

@@ -1,0 +1,174 @@
+from contextlib import ExitStack
+
+import concourse.mybir as mybir
+from concourse.masks import make_identity
+
+K, T, S, N = 512, 1024, 512, 512
+FLOPS = 2 * K * S * N
+
+F32 = mybir.dt.float32
+BF16 = mybir.dt.bfloat16
+I32 = mybir.dt.int32
+U32 = mybir.dt.uint32
+U16 = mybir.dt.uint16
+U8 = mybir.dt.uint8
+FP8X4 = mybir.dt.float8_e4m3fn_x4
+MULT = mybir.AluOpType.mult
+
+P = 128
+PACK = 4
+HALF = S // 2
+LIST_ROWS = 16
+
+
+def tile_picked_tokscale_none_lo_kernel(tc, xT, tscale, cscale, w1, offs, out_0, out_1, out_2):
+    nc = tc.nc
+    with ExitStack() as ctx:
+        sb = ctx.enter_context(tc.tile_pool(name="sb", bufs=1))
+        psum = ctx.enter_context(tc.psum_pool(name="psum", bufs=8))
+
+        x_rows = xT.rearrange("(p j) t -> p j t", j=PACK)
+        w_rows = w1.rearrange("(p j) m -> p j m", j=PACK)
+
+        def load_x(pair, c0, c1):
+            raw = sb.tile([P, 2, c1 - c0], F32, name=f"x_raw_{pair}_{c0}")
+            nc.sync.dma_start(out=raw[:], in_=x_rows[:, 2 * pair : 2 * pair + 2, c0:c1])
+            return raw
+
+        ts_cols = sb.tile([P, 2, PACK], F32)
+        nc.scalar.dma_start(out=ts_cols[:], in_=tscale[0].rearrange("(b n i) -> n b i", b=2, i=PACK))
+        cs = sb.tile([P, PACK], F32)
+        nc.scalar.dma_start(out=cs[:], in_=cscale.rearrange("(p t) o -> p (t o)", t=PACK))
+
+        xa0 = load_x(0, 0, 512)
+        offsets = sb.tile([P, S // LIST_ROWS], U16)
+        nc.sync.dma_start(offsets[:], offs)
+        xa1 = load_x(0, 512, 1024)
+        xb0 = load_x(1, 0, 512)
+        xb1 = load_x(1, 512, 1024)
+        w_raw = []
+        for h in range(2):
+            raw = sb.tile([P, PACK, N // 2], F32, name=f"w_raw_{h}")
+            nc.sync.dma_start(out=raw[:], in_=w_rows[:, :, h * (N // 2) : (h + 1) * (N // 2)])
+            w_raw.append(raw)
+
+        ident = sb.tile([P, P], F32)
+        make_identity(nc, ident[:])
+
+        pairs = [sb.tile([P, T], U32, name=f"x_pairs_{a}", align_bytes=64) for a in range(2)]
+
+        def cast_x(copy, pair, raw, c0, lo, hi):
+            dst = pairs[pair][:].bitcast(BF16).rearrange("p (n j) -> p n j", j=2)
+            copy(dst[:, c0 + lo : c0 + hi, :], raw[:, :, lo:hi].rearrange("p j n -> p n j"))
+
+        ts_window = sb.tile([P, T], F32, align_bytes=64)
+        ts_banks = []
+        for b in range(2):
+            bank = psum.tile([P, PACK, P], F32, name=f"ts_bank_{b}", tag="bank")
+            for i in range(PACK):
+                nc.tensor.transpose(bank[:, i, :], ts_cols[:, b, i : i + 1].to_broadcast([P, P]), ident[:])
+            ts_banks.append(bank)
+
+        def spread_ts(copy, b):
+            dst = ts_window[:, b * 512 : (b + 1) * 512].rearrange("p (n i) -> p n i", i=PACK)
+            copy(dst, ts_banks[b][:].rearrange("p i n -> p n i"))
+
+        cast_x(nc.vector.tensor_copy, 0, xa0, 0, 0, 512)
+        spread_ts(nc.vector.tensor_copy, 0)
+        spread_ts(nc.scalar.copy, 1)
+        cast_x(nc.vector.tensor_copy, 0, xa1, 512, 0, 320)
+        cast_x(nc.scalar.copy, 0, xa1, 512, 320, 512)
+
+        tg = sb.tile([P, S], F32, align_bytes=64)
+        nc.vector.tensor_copy(tg[:], ts_window[:].indirect(offsets[:]))
+
+        x_picked = [sb.tile([P, HALF, 2], U32, name=f"x_picked_{h}", align_bytes=64) for h in range(2)]
+        list_cols = HALF // LIST_ROWS
+
+        def gather_x(pair, h):
+            nc.vector.tensor_copy(
+                x_picked[h][:, :, pair],
+                pairs[pair][:].indirect(offsets[:, h * list_cols : (h + 1) * list_cols]),
+            )
+
+        cast_x(nc.scalar.copy, 1, xb0, 0, 0, 512)
+        gather_x(0, 0)
+        gather_x(0, 1)
+        cast_x(nc.scalar.copy, 1, xb1, 512, 0, 512)
+        gather_x(1, 0)
+        gather_x(1, 1)
+
+        w_dealt = sb.tile([P, PACK * P * PACK], BF16, align_bytes=64)
+
+        def cast_w(copy, h, lo, hi):
+            dst = w_dealt[:].rearrange("p (t m j) -> p m t j", t=PACK, j=PACK)
+            src = w_raw[h][:].rearrange("p j (m t) -> p m t j", t=PACK)
+            copy(dst[:, 64 * h + lo : 64 * h + hi], src[:, lo:hi])
+
+        cast_w(nc.scalar.copy, 0, 0, 64)
+
+        x_codes = [sb.tile([P, HALF], U32, name=f"x_codes_{h}", align_bytes=64) for h in range(2)]
+        x_scales = [sb.tile([P, HALF], U8, name=f"x_scales_{h}", align_bytes=64) for h in range(2)]
+        for h in range(2):
+            nc.vector.quantize_mx(
+                out=x_codes[h][:].bitcast(FP8X4),
+                scales=x_scales[h][:],
+                in_=x_picked[h][:].rearrange("p s a -> p (s a)").bitcast(BF16),
+            )
+
+        cast_w(nc.scalar.copy, 1, 0, 44)
+        cast_w(nc.vector.tensor_copy, 1, 44, 64)
+
+        w_codes = [sb.tile([P, P], U32, name=f"w_codes_{t}", align_bytes=64) for t in range(PACK)]
+        w_scales = [sb.tile([P, P], U8, name=f"w_scales_{t}", align_bytes=64) for t in range(PACK)]
+        for t in range(PACK):
+            nc.vector.quantize_mx(
+                out=w_codes[t][:].bitcast(FP8X4),
+                scales=w_scales[t][:],
+                in_=w_dealt[:, t * 512 : (t + 1) * 512],
+            )
+
+        out_rows = out_0.rearrange("(p t) s -> p t s", t=PACK)
+        out_words = out_1[0].rearrange("p s r -> p (s r)").bitcast(I32)
+        out_scales = out_2[0].bitcast(I32)
+        y_scales = sb.tile([P, S], U8, align_bytes=64)
+        y = [sb.tile([P, PACK, HALF], F32, name=f"y_{h}", align_bytes=64) for h in range(2)]
+        y_rounded = [sb.tile([P, HALF * PACK], BF16, name=f"y_rounded_{h}", align_bytes=64) for h in range(2)]
+        y_codes = [sb.tile([P, HALF], U32, name=f"y_codes_{h}", align_bytes=64) for h in range(2)]
+
+        def product(h):
+            cols = slice(h * HALF, (h + 1) * HALF)
+            for t in range(PACK):
+                acc = psum.tile([P, HALF], F32, name=f"acc_{h}_{t}", tag="bank")
+                nc.tensor.matmul_mx(
+                    out=acc[:],
+                    lhsT=w_codes[t][:].bitcast(FP8X4),
+                    lhsT_scale=w_scales[t][:],
+                    rhs=x_codes[h][:].bitcast(FP8X4),
+                    rhs_scale=x_scales[h][:],
+                    start=True,
+                    stop=True,
+                )
+                nc.vector.scalar_tensor_tensor(y[h][:, t, :], acc[:], cs[:, t : t + 1], tg[:, cols], MULT, MULT)
+                if t % 2 == 1:
+                    nc.sync.dma_start(out=out_rows[:, t - 1 : t + 1, cols], in_=y[h][:, t - 1 : t + 1, :])
+
+        def round_y(copy, h, lo, hi):
+            dst = y_rounded[h][:].rearrange("p (s t) -> p s t", t=PACK)
+            copy(dst[:, lo:hi, :], y[h][:, :, lo:hi].rearrange("p t s -> p s t"))
+
+        def quantize_y(h):
+            cols = slice(h * HALF, (h + 1) * HALF)
+            nc.vector.quantize_mx(out=y_codes[h][:].bitcast(FP8X4), scales=y_scales[:, cols], in_=y_rounded[h][:])
+            nc.sync.dma_start(out=out_words[:, cols], in_=y_codes[h][:].bitcast(I32))
+
+        product(0)
+        round_y(nc.scalar.copy, 0, 0, HALF)
+        product(1)
+        round_y(nc.vector.tensor_copy, 1, 0, 160)
+        round_y(nc.scalar.copy, 1, 160, HALF)
+        quantize_y(0)
+        quantize_y(1)
+        for q in range(4):
+            queue = nc.scalar if q < 2 else nc.sync
+            queue.dma_start(out=out_scales[4 * q : 4 * q + 4, :], in_=y_scales[:].bitcast(I32)[32 * q : 32 * q + 4, :])

@@ -35,22 +35,18 @@ def tile_picked_tokscale_none_lo_kernel(tc, xT, tscale, cscale, w1, offs, out_0,
             nc.sync.dma_start(out=raw[:], in_=x_rows[:, 2 * pair : 2 * pair + 2, c0:c1])
             return raw
 
-        ts_cols = sb.tile([P, 2, PACK], F32)
-        nc.scalar.dma_start(out=ts_cols[:], in_=tscale[0].rearrange("(b n i) -> n b i", b=2, i=PACK))
-        cs = sb.tile([P, PACK], F32)
-        nc.scalar.dma_start(out=cs[:], in_=cscale.rearrange("(p t) o -> p (t o)", t=PACK))
-
-        xa0 = load_x(0, 0, 512)
         offsets = sb.tile([P, S // LIST_ROWS], U16)
         nc.sync.dma_start(offsets[:], offs)
-        xa1 = load_x(0, 512, 1024)
+        ts_window = sb.tile([P, T], F32, align_bytes=64)
+        nc.vector.memset(ts_window[0 : P - 1, :], 0.0)
+        nc.sync.dma_start(out=ts_window[P - 1 : P, :], in_=tscale[0:1, :])
+        xa = load_x(0, 0, T)
         xb0 = load_x(1, 0, 512)
         xb1 = load_x(1, 512, 1024)
-        w_raw = []
-        for h in range(2):
-            raw = sb.tile([P, PACK, N // 2], F32, name=f"w_raw_{h}")
-            nc.sync.dma_start(out=raw[:], in_=w_rows[:, :, h * (N // 2) : (h + 1) * (N // 2)])
-            w_raw.append(raw)
+        w_raw = sb.tile([P, PACK, N], F32)
+        nc.sync.dma_start(out=w_raw[:], in_=w_rows)
+        cs = sb.tile([P, PACK], F32)
+        nc.sync.dma_start(out=cs[:], in_=cscale.rearrange("(p t) o -> p (t o)", t=PACK))
 
         ident = sb.tile([P, P], F32)
         make_identity(nc, ident[:])
@@ -61,26 +57,20 @@ def tile_picked_tokscale_none_lo_kernel(tc, xT, tscale, cscale, w1, offs, out_0,
             dst = pairs[pair][:].bitcast(BF16).rearrange("p (n j) -> p n j", j=2)
             copy(dst[:, c0 + lo : c0 + hi, :], raw[:, :, lo:hi].rearrange("p j n -> p n j"))
 
-        ts_window = sb.tile([P, T], F32, align_bytes=64)
-        ts_banks = []
-        for b in range(2):
-            bank = psum.tile([P, PACK, P], F32, name=f"ts_bank_{b}", tag="bank")
-            for i in range(PACK):
-                nc.tensor.transpose(bank[:, i, :], ts_cols[:, b, i : i + 1].to_broadcast([P, P]), ident[:])
-            ts_banks.append(bank)
+        tg_row = sb.tile([P, S], F32, align_bytes=64)
+        nc.vector.tensor_copy(tg_row[:], ts_window[:].indirect(offsets[:]))
+        turned = psum.tile([P, PACK, P], F32, tag="bank")
+        for b in range(PACK):
+            nc.tensor.transpose(turned[:, b, :], tg_row[:, b * P : (b + 1) * P], ident[:])
 
-        def spread_ts(copy, b):
-            dst = ts_window[:, b * 512 : (b + 1) * 512].rearrange("p (n i) -> p n i", i=PACK)
-            copy(dst, ts_banks[b][:].rearrange("p i n -> p n i"))
+        cast_x(nc.vector.tensor_copy, 0, xa, 0, 0, 672)
+        cast_x(nc.scalar.copy, 0, xa, 0, 672, T)
 
-        cast_x(nc.vector.tensor_copy, 0, xa0, 0, 0, 512)
-        spread_ts(nc.vector.tensor_copy, 0)
-        spread_ts(nc.scalar.copy, 1)
-        cast_x(nc.vector.tensor_copy, 0, xa1, 512, 0, 320)
-        cast_x(nc.scalar.copy, 0, xa1, 512, 320, 512)
-
-        tg = sb.tile([P, S], F32, align_bytes=64)
-        nc.vector.tensor_copy(tg[:], ts_window[:].indirect(offsets[:]))
+        tg_cols = sb.tile([P, PACK], F32)
+        nc.scalar.copy(tg_cols[:], turned[:, :, P - 1])
+        spread = psum.tile([P, PACK, P], F32, tag="bank")
+        for b in range(PACK):
+            nc.tensor.transpose(spread[:, b, :], tg_cols[:, b : b + 1].to_broadcast([P, P]), ident[:])
 
         x_picked = [sb.tile([P, HALF, 2], U32, name=f"x_picked_{h}", align_bytes=64) for h in range(2)]
         list_cols = HALF // LIST_ROWS
@@ -94,18 +84,19 @@ def tile_picked_tokscale_none_lo_kernel(tc, xT, tscale, cscale, w1, offs, out_0,
         cast_x(nc.scalar.copy, 1, xb0, 0, 0, 512)
         gather_x(0, 0)
         gather_x(0, 1)
-        cast_x(nc.scalar.copy, 1, xb1, 512, 0, 512)
+        cast_x(nc.vector.tensor_copy, 1, xb1, 512, 0, 320)
+        cast_x(nc.scalar.copy, 1, xb1, 512, 320, 512)
         gather_x(1, 0)
         gather_x(1, 1)
+        tg = sb.tile([P, S], F32, align_bytes=64)
+        nc.scalar.copy(tg[:], spread[:].rearrange("p b n -> p (b n)"))
 
         w_dealt = sb.tile([P, PACK * P * PACK], BF16, align_bytes=64)
 
-        def cast_w(copy, h, lo, hi):
+        def cast_w(copy, lo, hi):
             dst = w_dealt[:].rearrange("p (t m j) -> p m t j", t=PACK, j=PACK)
-            src = w_raw[h][:].rearrange("p j (m t) -> p m t j", t=PACK)
-            copy(dst[:, 64 * h + lo : 64 * h + hi], src[:, lo:hi])
-
-        cast_w(nc.scalar.copy, 0, 0, 64)
+            src = w_raw[:].rearrange("p j (m t) -> p m t j", t=PACK)
+            copy(dst[:, lo:hi], src[:, lo:hi])
 
         x_codes = [sb.tile([P, HALF], U32, name=f"x_codes_{h}", align_bytes=64) for h in range(2)]
         x_scales = [sb.tile([P, HALF], U8, name=f"x_scales_{h}", align_bytes=64) for h in range(2)]
@@ -116,8 +107,8 @@ def tile_picked_tokscale_none_lo_kernel(tc, xT, tscale, cscale, w1, offs, out_0,
                 in_=x_picked[h][:].rearrange("p s a -> p (s a)").bitcast(BF16),
             )
 
-        cast_w(nc.scalar.copy, 1, 0, 44)
-        cast_w(nc.vector.tensor_copy, 1, 44, 64)
+        cast_w(nc.scalar.copy, 0, 64)
+        cast_w(nc.vector.tensor_copy, 64, P)
 
         w_codes = [sb.tile([P, P], U32, name=f"w_codes_{t}", align_bytes=64) for t in range(PACK)]
         w_scales = [sb.tile([P, P], U8, name=f"w_scales_{t}", align_bytes=64) for t in range(PACK)]
@@ -165,9 +156,9 @@ def tile_picked_tokscale_none_lo_kernel(tc, xT, tscale, cscale, w1, offs, out_0,
         product(0)
         round_y(nc.scalar.copy, 0, 0, HALF)
         product(1)
-        round_y(nc.vector.tensor_copy, 1, 0, 160)
-        round_y(nc.scalar.copy, 1, 160, HALF)
         quantize_y(0)
+        round_y(nc.vector.tensor_copy, 1, 0, 128)
+        round_y(nc.scalar.copy, 1, 128, HALF)
         quantize_y(1)
         for q in range(4):
             queue = nc.scalar if q < 2 else nc.sync

@@ -19,6 +19,9 @@ P = 128
 PACK = 4
 HALF = S // 2
 LIST_ROWS = 16
+X_LOADS = [[0,0,512,320],[0,512,1024,320],[1,0,256,0],[1,256,512,0],[1,512,768,0],[1,768,1024,160]]
+W_LOADS = [[0,64,0],[64,128,36]]
+Y_VECTOR = 128
 
 
 def tile_picked_tokscale_none_lo_kernel(tc, xT, tscale, cscale, w1, offs, out_0, out_1, out_2):
@@ -30,21 +33,21 @@ def tile_picked_tokscale_none_lo_kernel(tc, xT, tscale, cscale, w1, offs, out_0,
         x_rows = xT.rearrange("(p j) t -> p j t", j=PACK)
         w_rows = w1.rearrange("(p j) m -> p j m", j=PACK)
 
-        def load_x(pair, c0, c1):
-            raw = sb.tile([P, 2, c1 - c0], F32, name=f"x_raw_{pair}_{c0}")
-            nc.sync.dma_start(out=raw[:], in_=x_rows[:, 2 * pair : 2 * pair + 2, c0:c1])
-            return raw
-
         offsets = sb.tile([P, S // LIST_ROWS], U16)
         nc.sync.dma_start(offsets[:], offs)
         ts_window = sb.tile([P, T], F32, align_bytes=64)
         nc.vector.memset(ts_window[0 : P - 1, :], 0.0)
-        nc.sync.dma_start(out=ts_window[P - 1 : P, :], in_=tscale[0:1, :])
-        xa = load_x(0, 0, T)
-        xb0 = load_x(1, 0, 512)
-        xb1 = load_x(1, 512, 1024)
-        w_raw = sb.tile([P, PACK, N], F32)
-        nc.sync.dma_start(out=w_raw[:], in_=w_rows)
+        nc.scalar.dma_start(out=ts_window[P - 1 : P, :], in_=tscale[0:1, :])
+        x_raw = []
+        for pair, c0, c1, share in X_LOADS:
+            raw = sb.tile([P, 2, c1 - c0], F32, name=f"x_raw_{pair}_{c0}")
+            nc.sync.dma_start(out=raw[:], in_=x_rows[:, 2 * pair : 2 * pair + 2, c0:c1])
+            x_raw.append(raw)
+        w_raw = []
+        for m0, m1, share in W_LOADS:
+            raw = sb.tile([P, PACK, PACK * (m1 - m0)], F32, name=f"w_raw_{m0}", tag=f"w_raw_{m0}", align_bytes=64)
+            nc.sync.dma_start(out=raw[:], in_=w_rows[:, :, PACK * m0 : PACK * m1])
+            w_raw.append(raw)
         cs = sb.tile([P, PACK], F32)
         nc.sync.dma_start(out=cs[:], in_=cscale.rearrange("(p t) o -> p (t o)", t=PACK))
 
@@ -53,9 +56,15 @@ def tile_picked_tokscale_none_lo_kernel(tc, xT, tscale, cscale, w1, offs, out_0,
 
         pairs = [sb.tile([P, T], U32, name=f"x_pairs_{a}", align_bytes=64) for a in range(2)]
 
-        def cast_x(copy, pair, raw, c0, lo, hi):
-            dst = pairs[pair][:].bitcast(BF16).rearrange("p (n j) -> p n j", j=2)
-            copy(dst[:, c0 + lo : c0 + hi, :], raw[:, :, lo:hi].rearrange("p j n -> p n j"))
+        def shared(share, width):
+            return [(copy, lo, hi) for copy, lo, hi in ((nc.vector.tensor_copy, 0, share), (nc.scalar.copy, share, width)) if hi > lo]
+
+        def cast_x(which):
+            for raw, (pair, c0, c1, share) in zip(x_raw, X_LOADS):
+                if pair == which:
+                    dst = pairs[pair][:].bitcast(BF16).rearrange("p (n j) -> p n j", j=2)
+                    for copy, lo, hi in shared(share, c1 - c0):
+                        copy(dst[:, c0 + lo : c0 + hi, :], raw[:, :, lo:hi].rearrange("p j n -> p n j"))
 
         tg_row = sb.tile([P, S], F32, align_bytes=64)
         nc.vector.tensor_copy(tg_row[:], ts_window[:].indirect(offsets[:]))
@@ -63,8 +72,7 @@ def tile_picked_tokscale_none_lo_kernel(tc, xT, tscale, cscale, w1, offs, out_0,
         for b in range(PACK):
             nc.tensor.transpose(turned[:, b, :], tg_row[:, b * P : (b + 1) * P], ident[:])
 
-        cast_x(nc.vector.tensor_copy, 0, xa, 0, 0, 672)
-        cast_x(nc.scalar.copy, 0, xa, 0, 672, T)
+        cast_x(0)
 
         tg_cols = sb.tile([P, PACK], F32)
         nc.scalar.copy(tg_cols[:], turned[:, :, P - 1])
@@ -81,34 +89,36 @@ def tile_picked_tokscale_none_lo_kernel(tc, xT, tscale, cscale, w1, offs, out_0,
                 pairs[pair][:].indirect(offsets[:, h * list_cols : (h + 1) * list_cols]),
             )
 
-        cast_x(nc.scalar.copy, 1, xb0, 0, 0, 512)
         gather_x(0, 0)
         gather_x(0, 1)
-        cast_x(nc.vector.tensor_copy, 1, xb1, 512, 0, 320)
-        cast_x(nc.scalar.copy, 1, xb1, 512, 320, 512)
+        cast_x(1)
         gather_x(1, 0)
         gather_x(1, 1)
-        tg = sb.tile([P, S], F32, align_bytes=64)
-        nc.scalar.copy(tg[:], spread[:].rearrange("p b n -> p (b n)"))
 
-        w_dealt = sb.tile([P, PACK * P * PACK], BF16, align_bytes=64)
+        x_codes, x_scales = [], []
 
-        def cast_w(copy, lo, hi):
-            dst = w_dealt[:].rearrange("p (t m j) -> p m t j", t=PACK, j=PACK)
-            src = w_raw[:].rearrange("p j (m t) -> p m t j", t=PACK)
-            copy(dst[:, lo:hi], src[:, lo:hi])
-
-        x_codes = [sb.tile([P, HALF], U32, name=f"x_codes_{h}", align_bytes=64) for h in range(2)]
-        x_scales = [sb.tile([P, HALF], U8, name=f"x_scales_{h}", align_bytes=64) for h in range(2)]
-        for h in range(2):
+        def quantize_x(h, tag):
+            codes = sb.tile([P, HALF], U32, name=f"x_codes_{h}", tag=tag, align_bytes=64)
+            scales = sb.tile([P, HALF], U8, name=f"x_scales_{h}", align_bytes=64)
             nc.vector.quantize_mx(
-                out=x_codes[h][:].bitcast(FP8X4),
-                scales=x_scales[h][:],
+                out=codes[:].bitcast(FP8X4),
+                scales=scales[:],
                 in_=x_picked[h][:].rearrange("p s a -> p (s a)").bitcast(BF16),
             )
+            x_codes.append(codes)
+            x_scales.append(scales)
 
-        cast_w(nc.scalar.copy, 0, 64)
-        cast_w(nc.vector.tensor_copy, 64, P)
+        quantize_x(0, "x_codes_0")
+
+        w_dealt = sb.tile([P, PACK * P * PACK], BF16, tag="w_dealt", align_bytes=64)
+        for raw, (m0, m1, share) in zip(w_raw, W_LOADS):
+            dst = w_dealt[:].rearrange("p (t m j) -> p m t j", t=PACK, j=PACK)
+            src = raw[:].rearrange("p j (m t) -> p m t j", t=PACK)
+            for copy, lo, hi in shared(share, m1 - m0):
+                copy(dst[:, m0 + lo : m0 + hi], src[:, lo:hi])
+
+        tg = sb.tile([P, S], F32, tag=f"w_raw_{W_LOADS[-1][0]}", align_bytes=64)
+        nc.scalar.copy(tg[:], spread[:].rearrange("p b n -> p (b n)"))
 
         w_codes = [sb.tile([P, P], U32, name=f"w_codes_{t}", align_bytes=64) for t in range(PACK)]
         w_scales = [sb.tile([P, P], U8, name=f"w_scales_{t}", align_bytes=64) for t in range(PACK)]
@@ -118,6 +128,8 @@ def tile_picked_tokscale_none_lo_kernel(tc, xT, tscale, cscale, w1, offs, out_0,
                 scales=w_scales[t][:],
                 in_=w_dealt[:, t * 512 : (t + 1) * 512],
             )
+
+        quantize_x(1, "w_dealt")
 
         out_rows = out_0.rearrange("(p t) s -> p t s", t=PACK)
         out_words = out_1[0].rearrange("p s r -> p (s r)").bitcast(I32)
@@ -144,9 +156,10 @@ def tile_picked_tokscale_none_lo_kernel(tc, xT, tscale, cscale, w1, offs, out_0,
                 if t % 2 == 1:
                     nc.sync.dma_start(out=out_rows[:, t - 1 : t + 1, cols], in_=y[h][:, t - 1 : t + 1, :])
 
-        def round_y(copy, h, lo, hi):
+        def round_y(h, share):
             dst = y_rounded[h][:].rearrange("p (s t) -> p s t", t=PACK)
-            copy(dst[:, lo:hi, :], y[h][:, :, lo:hi].rearrange("p t s -> p s t"))
+            for copy, lo, hi in shared(share, HALF):
+                copy(dst[:, lo:hi, :], y[h][:, :, lo:hi].rearrange("p t s -> p s t"))
 
         def quantize_y(h):
             cols = slice(h * HALF, (h + 1) * HALF)
@@ -154,11 +167,10 @@ def tile_picked_tokscale_none_lo_kernel(tc, xT, tscale, cscale, w1, offs, out_0,
             nc.sync.dma_start(out=out_words[:, cols], in_=y_codes[h][:].bitcast(I32))
 
         product(0)
-        round_y(nc.scalar.copy, 0, 0, HALF)
+        round_y(0, 0)
         product(1)
         quantize_y(0)
-        round_y(nc.vector.tensor_copy, 1, 0, 128)
-        round_y(nc.scalar.copy, 1, 128, HALF)
+        round_y(1, Y_VECTOR)
         quantize_y(1)
         for q in range(4):
             queue = nc.scalar if q < 2 else nc.sync

@@ -21,7 +21,7 @@ HALF = S // 2
 LIST_ROWS = 16
 X_LOADS = [[0,0,512,320],[0,512,1024,320],[1,0,256,0],[1,256,512,0],[1,512,768,0],[1,768,1024,160]]
 W_LOADS = [[0,64,0],[64,128,36]]
-Y_VECTOR = 128
+Y_VECTOR = 192
 
 
 def tile_picked_tokscale_none_lo_kernel(tc, xT, tscale, cscale, w1, offs, out_0, out_1, out_2):
@@ -112,8 +112,8 @@ def tile_picked_tokscale_none_lo_kernel(tc, xT, tscale, cscale, w1, offs, out_0,
 
         w_dealt = sb.tile([P, PACK * P * PACK], BF16, tag="w_dealt", align_bytes=64)
         for raw, (m0, m1, share) in zip(w_raw, W_LOADS):
-            dst = w_dealt[:].rearrange("p (t m j) -> p m t j", t=PACK, j=PACK)
-            src = raw[:].rearrange("p j (m t) -> p m t j", t=PACK)
+            dst = w_dealt[:].rearrange("p (t m j) -> p m j t", t=PACK, j=PACK)
+            src = raw[:].rearrange("p j (m t) -> p m j t", t=PACK)
             for copy, lo, hi in shared(share, m1 - m0):
                 copy(dst[:, m0 + lo : m0 + hi], src[:, lo:hi])
 
@@ -122,7 +122,7 @@ def tile_picked_tokscale_none_lo_kernel(tc, xT, tscale, cscale, w1, offs, out_0,
 
         w_codes = [sb.tile([P, P], U32, name=f"w_codes_{t}", align_bytes=64) for t in range(PACK)]
         w_scales = [sb.tile([P, P], U8, name=f"w_scales_{t}", align_bytes=64) for t in range(PACK)]
-        for t in range(PACK):
+        for t in (0, 2, 3, 1):
             nc.vector.quantize_mx(
                 out=w_codes[t][:].bitcast(FP8X4),
                 scales=w_scales[t][:],
@@ -141,7 +141,7 @@ def tile_picked_tokscale_none_lo_kernel(tc, xT, tscale, cscale, w1, offs, out_0,
 
         def product(h):
             cols = slice(h * HALF, (h + 1) * HALF)
-            for t in range(PACK):
+            for t in (0, 2, 3, 1):
                 acc = psum.tile([P, HALF], F32, name=f"acc_{h}_{t}", tag="bank")
                 nc.tensor.matmul_mx(
                     out=acc[:],
@@ -152,14 +152,20 @@ def tile_picked_tokscale_none_lo_kernel(tc, xT, tscale, cscale, w1, offs, out_0,
                     start=True,
                     stop=True,
                 )
-                nc.vector.scalar_tensor_tensor(y[h][:, t, :], acc[:], cs[:, t : t + 1], tg[:, cols], MULT, MULT)
+                if (h, t) in ((0, 0), (1, 0)):
+                    scaled = sb.tile([P, HALF], F32, name=f"scaled_{h}_{t}")
+                    nc.scalar.activation(scaled[:], acc[:], mybir.ActivationFunctionType.Copy, scale=cs[:, t : t + 1])
+                    nc.gpsimd.tensor_tensor(y[h][:, t, :], scaled[:], tg[:, cols], MULT)
+                else:
+                    nc.vector.scalar_tensor_tensor(y[h][:, t, :], acc[:], cs[:, t : t + 1], tg[:, cols], MULT, MULT)
                 if t % 2 == 1:
                     nc.sync.dma_start(out=out_rows[:, t - 1 : t + 1, cols], in_=y[h][:, t - 1 : t + 1, :])
 
         def round_y(h, share):
-            dst = y_rounded[h][:].rearrange("p (s t) -> p s t", t=PACK)
-            for copy, lo, hi in shared(share, HALF):
-                copy(dst[:, lo:hi, :], y[h][:, :, lo:hi].rearrange("p t s -> p s t"))
+            dst = y_rounded[h][:].rearrange("p (c i t) -> p c t i", i=PACK, t=PACK)
+            src = y[h][:].rearrange("p t (c i) -> p c t i", i=PACK)
+            for copy, lo, hi in shared(share // PACK, HALF // PACK):
+                copy(dst[:, lo:hi], src[:, lo:hi])
 
         def quantize_y(h):
             cols = slice(h * HALF, (h + 1) * HALF)
@@ -169,8 +175,8 @@ def tile_picked_tokscale_none_lo_kernel(tc, xT, tscale, cscale, w1, offs, out_0,
         product(0)
         round_y(0, 0)
         product(1)
-        quantize_y(0)
         round_y(1, Y_VECTOR)
+        quantize_y(0)
         quantize_y(1)
         for q in range(4):
             queue = nc.scalar if q < 2 else nc.sync

@@ -14,39 +14,57 @@ U16 = mybir.dt.uint16
 U8 = mybir.dt.uint8
 FP8X4 = mybir.dt.float8_e4m3fn_x4
 MULT = mybir.AluOpType.mult
+COPY = mybir.ActivationFunctionType.Copy
 
 P = 128
 PACK = 4
+LINE = 4
 HALF = S // 2
 LIST_ROWS = 16
-X_LOADS = [[0,0,512,320],[0,512,1024,320],[1,0,256,0],[1,256,512,0],[1,512,768,0],[1,768,1024,160]]
-W_LOADS = [[0,64,0],[64,128,36]]
+QUADRANT = 32
+SCALE_ROWS = 4
+PSUM_BANKS = 8
+
+X_LOADS = (
+    (0, 0, 512, 0),
+    (0, 512, 1024, 320),
+    (1, 0, 256, 0),
+    (1, 256, 512, 0),
+    (1, 512, 768, 0),
+    (1, 768, 1024, 160),
+)
+W_LOADS = ((0, 64, 0), (64, 128, 32))
 Y_VECTOR = 192
+SHARED_TILE = 0
+TILE_ORDER = (0, 2, 3, 1)
+STORE_AFTER = {2: (2, 3), 3: (3, 4), 1: (0, 2)}
 
 
 def tile_picked_tokscale_none_lo_kernel(tc, xT, tscale, cscale, w1, offs, out_0, out_1, out_2):
     nc = tc.nc
     with ExitStack() as ctx:
         sb = ctx.enter_context(tc.tile_pool(name="sb", bufs=1))
-        psum = ctx.enter_context(tc.psum_pool(name="psum", bufs=8))
+        psum = ctx.enter_context(tc.psum_pool(name="psum", bufs=PSUM_BANKS))
 
         x_rows = xT.rearrange("(p j) t -> p j t", j=PACK)
         w_rows = w1.rearrange("(p j) m -> p j m", j=PACK)
 
         offsets = sb.tile([P, S // LIST_ROWS], U16)
-        nc.sync.dma_start(offsets[:], offs)
         ts_window = sb.tile([P, T], F32, align_bytes=64)
         nc.vector.memset(ts_window[0 : P - 1, :], 0.0)
         nc.scalar.dma_start(out=ts_window[P - 1 : P, :], in_=tscale[0:1, :])
+
         x_raw = []
-        for pair, c0, c1, share in X_LOADS:
-            raw = sb.tile([P, 2, c1 - c0], F32, name=f"x_raw_{pair}_{c0}")
-            nc.sync.dma_start(out=raw[:], in_=x_rows[:, 2 * pair : 2 * pair + 2, c0:c1])
+        for pair, first, end, share in X_LOADS:
+            raw = sb.tile([P, 2, end - first], F32, name=f"x_raw_{pair}_{first}")
+            nc.sync.dma_start(out=raw[:], in_=x_rows[:, 2 * pair : 2 * pair + 2, first:end])
             x_raw.append(raw)
+            if len(x_raw) == 1:
+                nc.sync.dma_start(offsets[:], offs)
         w_raw = []
-        for m0, m1, share in W_LOADS:
-            raw = sb.tile([P, PACK, PACK * (m1 - m0)], F32, name=f"w_raw_{m0}", tag=f"w_raw_{m0}", align_bytes=64)
-            nc.sync.dma_start(out=raw[:], in_=w_rows[:, :, PACK * m0 : PACK * m1])
+        for first, end, share in W_LOADS:
+            raw = sb.tile([P, PACK, PACK * (end - first)], F32, name=f"w_raw_{first}", align_bytes=64)
+            nc.sync.dma_start(out=raw[:], in_=w_rows[:, :, PACK * first : PACK * end])
             w_raw.append(raw)
         cs = sb.tile([P, PACK], F32)
         nc.sync.dma_start(out=cs[:], in_=cscale.rearrange("(p t) o -> p (t o)", t=PACK))
@@ -54,46 +72,46 @@ def tile_picked_tokscale_none_lo_kernel(tc, xT, tscale, cscale, w1, offs, out_0,
         ident = sb.tile([P, P], F32)
         make_identity(nc, ident[:])
 
-        pairs = [sb.tile([P, T], U32, name=f"x_pairs_{a}", align_bytes=64) for a in range(2)]
-
         def shared(share, width):
-            return [(copy, lo, hi) for copy, lo, hi in ((nc.vector.tensor_copy, 0, share), (nc.scalar.copy, share, width)) if hi > lo]
+            parts = ((nc.vector.tensor_copy, 0, share), (nc.scalar.copy, share, width))
+            return [(copy, lo, hi) for copy, lo, hi in parts if hi > lo]
 
-        def cast_x(which):
-            for raw, (pair, c0, c1, share) in zip(x_raw, X_LOADS):
+        x_pairs = [sb.tile([P, T], U32, name=f"x_pairs_{a}", align_bytes=64) for a in range(2)]
+
+        def round_x(which):
+            for raw, (pair, first, end, share) in zip(x_raw, X_LOADS):
                 if pair == which:
-                    dst = pairs[pair][:].bitcast(BF16).rearrange("p (n j) -> p n j", j=2)
-                    for copy, lo, hi in shared(share, c1 - c0):
-                        copy(dst[:, c0 + lo : c0 + hi, :], raw[:, :, lo:hi].rearrange("p j n -> p n j"))
+                    dst = x_pairs[pair][:].bitcast(BF16).rearrange("p (n j) -> p n j", j=2)
+                    for copy, lo, hi in shared(share, end - first):
+                        copy(dst[:, first + lo : first + hi, :], raw[:, :, lo:hi].rearrange("p j n -> p n j"))
 
         tg_row = sb.tile([P, S], F32, align_bytes=64)
         nc.vector.tensor_copy(tg_row[:], ts_window[:].indirect(offsets[:]))
-        turned = psum.tile([P, PACK, P], F32, tag="bank")
-        for b in range(PACK):
+        turned = psum.tile([P, S // P, P], F32, tag="bank")
+        for b in range(S // P):
             nc.tensor.transpose(turned[:, b, :], tg_row[:, b * P : (b + 1) * P], ident[:])
 
-        cast_x(0)
+        round_x(0)
 
-        tg_cols = sb.tile([P, PACK], F32)
+        tg_cols = sb.tile([P, S // P], F32)
         nc.scalar.copy(tg_cols[:], turned[:, :, P - 1])
-        spread = psum.tile([P, PACK, P], F32, tag="bank")
-        for b in range(PACK):
+        spread = psum.tile([P, S // P, P], F32, tag="bank")
+        for b in range(S // P):
             nc.tensor.transpose(spread[:, b, :], tg_cols[:, b : b + 1].to_broadcast([P, P]), ident[:])
 
         x_picked = [sb.tile([P, HALF, 2], U32, name=f"x_picked_{h}", align_bytes=64) for h in range(2)]
         list_cols = HALF // LIST_ROWS
 
-        def gather_x(pair, h):
-            nc.vector.tensor_copy(
-                x_picked[h][:, :, pair],
-                pairs[pair][:].indirect(offsets[:, h * list_cols : (h + 1) * list_cols]),
-            )
+        def gather_x(pair):
+            for h in range(2):
+                nc.vector.tensor_copy(
+                    x_picked[h][:, :, pair],
+                    x_pairs[pair][:].indirect(offsets[:, h * list_cols : (h + 1) * list_cols]),
+                )
 
-        gather_x(0, 0)
-        gather_x(0, 1)
-        cast_x(1)
-        gather_x(1, 0)
-        gather_x(1, 1)
+        gather_x(0)
+        round_x(1)
+        gather_x(1)
 
         x_codes, x_scales = [], []
 
@@ -111,24 +129,23 @@ def tile_picked_tokscale_none_lo_kernel(tc, xT, tscale, cscale, w1, offs, out_0,
         quantize_x(0, "x_codes_0")
 
         w_dealt = sb.tile([P, PACK * P * PACK], BF16, tag="w_dealt", align_bytes=64)
-        for raw, (m0, m1, share) in zip(w_raw, W_LOADS):
+        for raw, (first, end, share) in zip(w_raw, W_LOADS):
             dst = w_dealt[:].rearrange("p (t m j) -> p m j t", t=PACK, j=PACK)
             src = raw[:].rearrange("p j (m t) -> p m j t", t=PACK)
-            for copy, lo, hi in shared(share, m1 - m0):
-                copy(dst[:, m0 + lo : m0 + hi], src[:, lo:hi])
+            for copy, lo, hi in shared(share, end - first):
+                copy(dst[:, first + lo : first + hi], src[:, lo:hi])
 
         tg = sb.tile([P, S], F32, tag=f"w_raw_{W_LOADS[-1][0]}", align_bytes=64)
         nc.scalar.copy(tg[:], spread[:].rearrange("p b n -> p (b n)"))
 
         w_codes = [sb.tile([P, P], U32, name=f"w_codes_{t}", align_bytes=64) for t in range(PACK)]
         w_scales = [sb.tile([P, P], U8, name=f"w_scales_{t}", align_bytes=64) for t in range(PACK)]
-        for t in (0, 2, 3, 1):
+        for t in TILE_ORDER:
             nc.vector.quantize_mx(
                 out=w_codes[t][:].bitcast(FP8X4),
                 scales=w_scales[t][:],
-                in_=w_dealt[:, t * 512 : (t + 1) * 512],
+                in_=w_dealt[:, t * P * PACK : (t + 1) * P * PACK],
             )
-
         quantize_x(1, "w_dealt")
 
         out_rows = out_0.rearrange("(p t) s -> p t s", t=PACK)
@@ -141,7 +158,7 @@ def tile_picked_tokscale_none_lo_kernel(tc, xT, tscale, cscale, w1, offs, out_0,
 
         def product(h):
             cols = slice(h * HALF, (h + 1) * HALF)
-            for t in (0, 2, 3, 1):
+            for t in TILE_ORDER:
                 acc = psum.tile([P, HALF], F32, name=f"acc_{h}_{t}", tag="bank")
                 nc.tensor.matmul_mx(
                     out=acc[:],
@@ -152,19 +169,20 @@ def tile_picked_tokscale_none_lo_kernel(tc, xT, tscale, cscale, w1, offs, out_0,
                     start=True,
                     stop=True,
                 )
-                if (h, t) in ((0, 0), (1, 0)):
-                    scaled = sb.tile([P, HALF], F32, name=f"scaled_{h}_{t}")
-                    nc.scalar.activation(scaled[:], acc[:], mybir.ActivationFunctionType.Copy, scale=cs[:, t : t + 1])
+                if t == SHARED_TILE:
+                    scaled = sb.tile([P, HALF], F32, name=f"scaled_{h}")
+                    nc.scalar.activation(scaled[:], acc[:], COPY, scale=cs[:, t : t + 1])
                     nc.gpsimd.tensor_tensor(y[h][:, t, :], scaled[:], tg[:, cols], MULT)
                 else:
                     nc.vector.scalar_tensor_tensor(y[h][:, t, :], acc[:], cs[:, t : t + 1], tg[:, cols], MULT, MULT)
-                if t % 2 == 1:
-                    nc.sync.dma_start(out=out_rows[:, t - 1 : t + 1, cols], in_=y[h][:, t - 1 : t + 1, :])
+                if t in STORE_AFTER:
+                    lo, hi = STORE_AFTER[t]
+                    nc.sync.dma_start(out=out_rows[:, lo:hi, cols], in_=y[h][:, lo:hi, :])
 
         def round_y(h, share):
-            dst = y_rounded[h][:].rearrange("p (c i t) -> p c t i", i=PACK, t=PACK)
-            src = y[h][:].rearrange("p t (c i) -> p c t i", i=PACK)
-            for copy, lo, hi in shared(share // PACK, HALF // PACK):
+            dst = y_rounded[h][:].rearrange("p (c i t) -> p c t i", i=LINE, t=PACK)
+            src = y[h][:].rearrange("p t (c i) -> p c t i", i=LINE)
+            for copy, lo, hi in shared(share // LINE, HALF // LINE):
                 copy(dst[:, lo:hi], src[:, lo:hi])
 
         def quantize_y(h):
@@ -178,6 +196,10 @@ def tile_picked_tokscale_none_lo_kernel(tc, xT, tscale, cscale, w1, offs, out_0,
         round_y(1, Y_VECTOR)
         quantize_y(0)
         quantize_y(1)
-        for q in range(4):
+
+        for q in range(P // QUADRANT):
             queue = nc.scalar if q < 2 else nc.sync
-            queue.dma_start(out=out_scales[4 * q : 4 * q + 4, :], in_=y_scales[:].bitcast(I32)[32 * q : 32 * q + 4, :])
+            queue.dma_start(
+                out=out_scales[SCALE_ROWS * q : SCALE_ROWS * (q + 1), :],
+                in_=y_scales[:].bitcast(I32)[QUADRANT * q : QUADRANT * q + SCALE_ROWS, :],
+            )

@@ -1,7 +1,6 @@
 from contextlib import ExitStack
 
 import concourse.mybir as mybir
-from concourse.masks import make_identity
 
 K, T, S, N = 512, 1024, 512, 512
 FLOPS = 2 * K * S * N
@@ -14,6 +13,8 @@ U16 = mybir.dt.uint16
 U8 = mybir.dt.uint8
 FP8X4 = mybir.dt.float8_e4m3fn_x4
 MULT = mybir.AluOpType.mult
+ADD = mybir.AluOpType.add
+EQUAL = mybir.AluOpType.is_equal
 COPY = mybir.ActivationFunctionType.Copy
 
 P = 128
@@ -26,18 +27,19 @@ SCALE_ROWS = 4
 PSUM_BANKS = 8
 
 X_LOADS = (
-    (0, 0, 512, 0),
+    (0, 0, 256, 0),
+    (0, 256, 512, 0),
     (0, 512, 1024, 320),
     (1, 0, 256, 0),
     (1, 256, 512, 0),
     (1, 512, 768, 0),
     (1, 768, 1024, 160),
 )
-W_LOADS = ((0, 64, 0), (64, 128, 32))
+W_LOADS = ((0, 32, 0), (32, 96, 28), (96, 128, 18))
 Y_VECTOR = 192
 SHARED_TILE = 0
 TILE_ORDER = (0, 2, 3, 1)
-STORE_AFTER = {2: (2, 3), 3: (3, 4), 1: (0, 2)}
+STORE_AFTER = ({2: (2, 3), 3: (3, 4), 1: (0, 2)}, {3: (2, 4), 1: (0, 2)})
 
 
 def tile_picked_tokscale_none_lo_kernel(tc, xT, tscale, cscale, w1, offs, out_0, out_1, out_2):
@@ -69,8 +71,16 @@ def tile_picked_tokscale_none_lo_kernel(tc, xT, tscale, cscale, w1, offs, out_0,
         cs = sb.tile([P, PACK], F32)
         nc.sync.dma_start(out=cs[:], in_=cscale.rearrange("(p t) o -> p (t o)", t=PACK))
 
+        ones = sb.tile([P, P], F32)
+        ramp = sb.tile([P, P], F32, align_bytes=64)
+        ramp_turned = sb.tile([P, P], F32, align_bytes=64)
         ident = sb.tile([P, P], F32)
-        make_identity(nc, ident[:])
+        nc.vector.memset(ones[:], 1.0)
+        nc.vector.tensor_tensor_scan(ramp[:], ones[:], ones[:], 0.0, MULT, ADD)
+        nc.vector.transpose(ramp_turned[:], ramp[:])
+        for q in range(0, P, QUADRANT):
+            rows = slice(q, q + QUADRANT)
+            nc.vector.tensor_scalar(ident[rows, :], ramp[rows, :], ramp_turned[rows, q : q + 1], None, EQUAL)
 
         def shared(share, width):
             parts = ((nc.vector.tensor_copy, 0, share), (nc.scalar.copy, share, width))
@@ -93,12 +103,6 @@ def tile_picked_tokscale_none_lo_kernel(tc, xT, tscale, cscale, w1, offs, out_0,
 
         round_x(0)
 
-        tg_cols = sb.tile([P, S // P], F32)
-        nc.scalar.copy(tg_cols[:], turned[:, :, P - 1])
-        spread = psum.tile([P, S // P, P], F32, tag="bank")
-        for b in range(S // P):
-            nc.tensor.transpose(spread[:, b, :], tg_cols[:, b : b + 1].to_broadcast([P, P]), ident[:])
-
         x_picked = [sb.tile([P, HALF, 2], U32, name=f"x_picked_{h}", align_bytes=64) for h in range(2)]
         list_cols = HALF // LIST_ROWS
 
@@ -111,6 +115,13 @@ def tile_picked_tokscale_none_lo_kernel(tc, xT, tscale, cscale, w1, offs, out_0,
 
         gather_x(0)
         round_x(1)
+
+        tg_cols = sb.tile([P, S // P], F32, tag="x_raw_1_0")
+        nc.scalar.copy(tg_cols[:], turned[:, :, P - 1])
+        spread = psum.tile([P, S // P, P], F32, tag="bank")
+        for b in range(S // P):
+            nc.tensor.transpose(spread[:, b, :], tg_cols[:, b : b + 1].to_broadcast([P, P]), ident[:])
+
         gather_x(1)
 
         x_codes, x_scales = [], []
@@ -175,8 +186,8 @@ def tile_picked_tokscale_none_lo_kernel(tc, xT, tscale, cscale, w1, offs, out_0,
                     nc.gpsimd.tensor_tensor(y[h][:, t, :], scaled[:], tg[:, cols], MULT)
                 else:
                     nc.vector.scalar_tensor_tensor(y[h][:, t, :], acc[:], cs[:, t : t + 1], tg[:, cols], MULT, MULT)
-                if t in STORE_AFTER:
-                    lo, hi = STORE_AFTER[t]
+                if t in STORE_AFTER[h]:
+                    lo, hi = STORE_AFTER[h][t]
                     nc.sync.dma_start(out=out_rows[:, lo:hi, cols], in_=y[h][:, lo:hi, :])
 
         def round_y(h, share):

@@ -35,7 +35,7 @@ X_LOADS = (
     (1, 512, 768, 0),
     (1, 768, 1024, 160),
 )
-W_LOADS = ((0, 32, 0), (32, 96, 28), (96, 128, 18))
+W_LOADS = ((0, 32, 0), (32, 64, 0), (64, 96, 8), (96, 128, 20))
 Y_VECTOR = 192
 SHARED_TILE = 0
 TILE_ORDER = (0, 2, 3, 1)

@@ -39,7 +39,7 @@ W_LOADS = ((0, 32, 0), (32, 64, 0), (64, 96, 8), (96, 128, 20))
 Y_VECTOR = 192
 SHARED_TILE = 0
 TILE_ORDER = (0, 2, 3, 1)
-STORE_AFTER = ({2: (2, 3), 3: (3, 4), 1: (0, 2)}, {3: (2, 4), 1: (0, 2)})
+STORE_AFTER = {2: (2, 3), 3: (3, 4), 1: (0, 2)}
 
 
 def tile_picked_tokscale_none_lo_kernel(tc, xT, tscale, cscale, w1, offs, out_0, out_1, out_2):
@@ -186,8 +186,8 @@ def tile_picked_tokscale_none_lo_kernel(tc, xT, tscale, cscale, w1, offs, out_0,
                     nc.gpsimd.tensor_tensor(y[h][:, t, :], scaled[:], tg[:, cols], MULT)
                 else:
                     nc.vector.scalar_tensor_tensor(y[h][:, t, :], acc[:], cs[:, t : t + 1], tg[:, cols], MULT, MULT)
-                if t in STORE_AFTER[h]:
-                    lo, hi = STORE_AFTER[h][t]
+                if t in STORE_AFTER:
+                    lo, hi = STORE_AFTER[t]
                     nc.sync.dma_start(out=out_rows[:, lo:hi, cols], in_=y[h][:, lo:hi, :])
 
         def round_y(h, share):

@@ -15,7 +15,6 @@ FP8X4 = mybir.dt.float8_e4m3fn_x4
 MULT = mybir.AluOpType.mult
 ADD = mybir.AluOpType.add
 EQUAL = mybir.AluOpType.is_equal
-COPY = mybir.ActivationFunctionType.Copy
 
 P = 128
 PACK = 4
@@ -27,8 +26,7 @@ SCALE_ROWS = 4
 PSUM_BANKS = 8
 
 X_LOADS = (
-    (0, 0, 256, 0),
-    (0, 256, 512, 0),
+    (0, 0, 512, 0),
     (0, 512, 1024, 320),
     (1, 0, 256, 0),
     (1, 256, 512, 0),
@@ -36,10 +34,8 @@ X_LOADS = (
     (1, 768, 1024, 160),
 )
 W_LOADS = ((0, 32, 0), (32, 64, 0), (64, 96, 8), (96, 128, 20))
-Y_VECTOR = 192
-SHARED_TILE = 0
-TILE_ORDER = (0, 2, 3, 1)
-STORE_AFTER = {2: (2, 3), 3: (3, 4), 1: (0, 2)}
+Y_VECTOR = 128
+STORE_AFTER = {0: (0, 1), 1: (1, 2), 3: (2, 4)}
 
 
 def tile_picked_tokscale_none_lo_kernel(tc, xT, tscale, cscale, w1, offs, out_0, out_1, out_2):
@@ -151,7 +147,7 @@ def tile_picked_tokscale_none_lo_kernel(tc, xT, tscale, cscale, w1, offs, out_0,
 
         w_codes = [sb.tile([P, P], U32, name=f"w_codes_{t}", align_bytes=64) for t in range(PACK)]
         w_scales = [sb.tile([P, P], U8, name=f"w_scales_{t}", align_bytes=64) for t in range(PACK)]
-        for t in TILE_ORDER:
+        for t in range(PACK):
             nc.vector.quantize_mx(
                 out=w_codes[t][:].bitcast(FP8X4),
                 scales=w_scales[t][:],
@@ -169,7 +165,7 @@ def tile_picked_tokscale_none_lo_kernel(tc, xT, tscale, cscale, w1, offs, out_0,
 
         def product(h):
             cols = slice(h * HALF, (h + 1) * HALF)
-            for t in TILE_ORDER:
+            for t in range(PACK):
                 acc = psum.tile([P, HALF], F32, name=f"acc_{h}_{t}", tag="bank")
                 nc.tensor.matmul_mx(
                     out=acc[:],
@@ -180,12 +176,7 @@ def tile_picked_tokscale_none_lo_kernel(tc, xT, tscale, cscale, w1, offs, out_0,
                     start=True,
                     stop=True,
                 )
-                if t == SHARED_TILE:
-                    scaled = sb.tile([P, HALF], F32, name=f"scaled_{h}")
-                    nc.scalar.activation(scaled[:], acc[:], COPY, scale=cs[:, t : t + 1])
-                    nc.gpsimd.tensor_tensor(y[h][:, t, :], scaled[:], tg[:, cols], MULT)
-                else:
-                    nc.vector.scalar_tensor_tensor(y[h][:, t, :], acc[:], cs[:, t : t + 1], tg[:, cols], MULT, MULT)
+                nc.vector.scalar_tensor_tensor(y[h][:, t, :], acc[:], cs[:, t : t + 1], tg[:, cols], MULT, MULT)
                 if t in STORE_AFTER:
                     lo, hi = STORE_AFTER[t]
                     nc.sync.dma_start(out=out_rows[:, lo:hi, cols], in_=y[h][:, lo:hi, :])
@@ -204,8 +195,8 @@ def tile_picked_tokscale_none_lo_kernel(tc, xT, tscale, cscale, w1, offs, out_0,
         product(0)
         round_y(0, 0)
         product(1)
-        round_y(1, Y_VECTOR)
         quantize_y(0)
+        round_y(1, Y_VECTOR)
         quantize_y(1)
 
         for q in range(P // QUADRANT):

@@ -33,7 +33,7 @@ X_LOADS = (
     (1, 512, 768, 0),
     (1, 768, 1024, 160),
 )
-W_LOADS = ((0, 32, 0), (32, 64, 0), (64, 96, 8), (96, 128, 20))
+W_LOADS = ((0, 64, 0), (64, 128, 40))
 Y_VECTOR = 128
 STORE_AFTER = {0: (0, 1), 1: (1, 2), 3: (2, 4)}
 
@@ -187,17 +187,23 @@ def tile_picked_tokscale_none_lo_kernel(tc, xT, tscale, cscale, w1, offs, out_0,
             for copy, lo, hi in shared(share // LINE, HALF // LINE):
                 copy(dst[:, lo:hi], src[:, lo:hi])
 
-        def quantize_y(h):
-            cols = slice(h * HALF, (h + 1) * HALF)
-            nc.vector.quantize_mx(out=y_codes[h][:].bitcast(FP8X4), scales=y_scales[:, cols], in_=y_rounded[h][:])
-            nc.sync.dma_start(out=out_words[:, cols], in_=y_codes[h][:].bitcast(I32))
+        def quantize_y(first, end):
+            h, at = divmod(first, HALF)
+            nc.vector.quantize_mx(
+                out=y_codes[h][:, at : at + end - first].bitcast(FP8X4),
+                scales=y_scales[:, first:end],
+                in_=y_rounded[h][:, PACK * at : PACK * (at + end - first)],
+            )
+            if end % HALF == 0:
+                nc.sync.dma_start(out=out_words[:, end - HALF : end], in_=y_codes[h][:].bitcast(I32))
 
         product(0)
         round_y(0, 0)
         product(1)
-        quantize_y(0)
+        quantize_y(0, HALF // 2)
         round_y(1, Y_VECTOR)
-        quantize_y(1)
+        quantize_y(HALF // 2, HALF)
+        quantize_y(HALF, S)
 
         for q in range(P // QUADRANT):
             queue = nc.scalar if q < 2 else nc.sync

@@ -15,6 +15,7 @@ FP8X4 = mybir.dt.float8_e4m3fn_x4
 MULT = mybir.AluOpType.mult
 ADD = mybir.AluOpType.add
 EQUAL = mybir.AluOpType.is_equal
+COPY = mybir.ActivationFunctionType.Copy
 
 P = 128
 PACK = 4
@@ -25,15 +26,8 @@ QUADRANT = 32
 SCALE_ROWS = 4
 PSUM_BANKS = 8
 
-X_LOADS = (
-    (0, 0, 512, 0),
-    (0, 512, 1024, 320),
-    (1, 0, 256, 0),
-    (1, 256, 512, 0),
-    (1, 512, 768, 0),
-    (1, 768, 1024, 160),
-)
-W_LOADS = ((0, 64, 0), (64, 128, 40))
+X_ORDER = (2, 0, 1, 3)
+W_LOADS = ((0, 56, 0), (56, 96, 40), (96, 128, 16))
 Y_VECTOR = 128
 STORE_AFTER = {0: (0, 1), 1: (1, 2), 3: (2, 4)}
 
@@ -52,13 +46,14 @@ def tile_picked_tokscale_none_lo_kernel(tc, xT, tscale, cscale, w1, offs, out_0,
         nc.vector.memset(ts_window[0 : P - 1, :], 0.0)
         nc.scalar.dma_start(out=ts_window[P - 1 : P, :], in_=tscale[0:1, :])
 
-        x_raw = []
-        for pair, first, end, share in X_LOADS:
-            raw = sb.tile([P, 2, end - first], F32, name=f"x_raw_{pair}_{first}")
-            nc.sync.dma_start(out=raw[:], in_=x_rows[:, 2 * pair : 2 * pair + 2, first:end])
-            x_raw.append(raw)
-            if len(x_raw) == 1:
-                nc.sync.dma_start(offsets[:], offs)
+        nc.sync.dma_start(offsets[:], offs)
+        x_planes = {}
+        for j in X_ORDER:
+            x_planes[j] = sb.tile([P, T], F32, name=f"x_plane_{j}", align_bytes=64)
+            pieces = 2 if j == X_ORDER[0] else 1
+            for i in range(pieces):
+                cols = slice(i * T // pieces, (i + 1) * T // pieces)
+                nc.sync.dma_start(out=x_planes[j][:, cols], in_=x_rows[:, j, cols])
         w_raw = []
         for first, end, share in W_LOADS:
             raw = sb.tile([P, PACK, PACK * (end - first)], F32, name=f"w_raw_{first}", align_bytes=64)
@@ -82,43 +77,38 @@ def tile_picked_tokscale_none_lo_kernel(tc, xT, tscale, cscale, w1, offs, out_0,
             parts = ((nc.vector.tensor_copy, 0, share), (nc.scalar.copy, share, width))
             return [(copy, lo, hi) for copy, lo, hi in parts if hi > lo]
 
-        x_pairs = [sb.tile([P, T], U32, name=f"x_pairs_{a}", align_bytes=64) for a in range(2)]
-
-        def round_x(which):
-            for raw, (pair, first, end, share) in zip(x_raw, X_LOADS):
-                if pair == which:
-                    dst = x_pairs[pair][:].bitcast(BF16).rearrange("p (n j) -> p n j", j=2)
-                    for copy, lo, hi in shared(share, end - first):
-                        copy(dst[:, first + lo : first + hi, :], raw[:, :, lo:hi].rearrange("p j n -> p n j"))
-
         tg_row = sb.tile([P, S], F32, align_bytes=64)
         nc.vector.tensor_copy(tg_row[:], ts_window[:].indirect(offsets[:]))
         turned = psum.tile([P, S // P, P], F32, tag="bank")
         for b in range(S // P):
             nc.tensor.transpose(turned[:, b, :], tg_row[:, b * P : (b + 1) * P], ident[:])
 
-        round_x(0)
+        plane_2 = sb.tile([P, T], BF16, tag="plane_2", align_bytes=64)
+        for i in range(2):
+            cols = slice(i * T // 2, (i + 1) * T // 2)
+            nc.scalar.copy(plane_2[:, cols], x_planes[2][:, cols])
 
-        x_picked = [sb.tile([P, HALF, 2], U32, name=f"x_picked_{h}", align_bytes=64) for h in range(2)]
-        list_cols = HALF // LIST_ROWS
+        x_rounded = sb.tile([P, S * PACK], BF16, align_bytes=64)
+        x_slots = x_rounded[:].rearrange("p (s j) -> p s j", j=PACK)
 
-        def gather_x(pair):
-            for h in range(2):
-                nc.vector.tensor_copy(
-                    x_picked[h][:, :, pair],
-                    x_pairs[pair][:].indirect(offsets[:, h * list_cols : (h + 1) * list_cols]),
-                )
+        def entries(h):
+            return offsets[:, h * HALF // LIST_ROWS : (h + 1) * HALF // LIST_ROWS]
 
-        gather_x(0)
-        round_x(1)
+        nc.scalar.activation(x_slots[:, :, 2], plane_2[:].indirect(offsets[:]), COPY)
 
-        tg_cols = sb.tile([P, S // P], F32, tag="x_raw_1_0")
-        nc.scalar.copy(tg_cols[:], turned[:, :, P - 1])
+        picked = sb.tile([P, 2, S], F32, align_bytes=64)
+        nc.vector.tensor_copy(picked[:, 0, :], x_planes[0][:].indirect(offsets[:]))
+        tg_cols = sb.tile([P, S // P], F32, tag="plane_2", align_bytes=64)
+        nc.vector.tensor_copy(tg_cols[:], turned[:, :, P - 1])
         spread = psum.tile([P, S // P, P], F32, tag="bank")
         for b in range(S // P):
             nc.tensor.transpose(spread[:, b, :], tg_cols[:, b : b + 1].to_broadcast([P, P]), ident[:])
-
-        gather_x(1)
+        for h in range(2):
+            cols = slice(h * HALF, (h + 1) * HALF)
+            nc.vector.tensor_copy(picked[:, 1, cols], x_planes[1][:].indirect(entries(h)))
+            nc.scalar.copy(x_slots[:, cols, 0:2], picked[:, :, cols].rearrange("p j s -> p s j"))
+        for h in range(2):
+            nc.vector.tensor_copy(x_slots[:, h * HALF : (h + 1) * HALF, 3], x_planes[3][:].indirect(entries(h)))
 
         x_codes, x_scales = [], []
 
@@ -128,7 +118,7 @@ def tile_picked_tokscale_none_lo_kernel(tc, xT, tscale, cscale, w1, offs, out_0,
             nc.vector.quantize_mx(
                 out=codes[:].bitcast(FP8X4),
                 scales=scales[:],
-                in_=x_picked[h][:].rearrange("p s a -> p (s a)").bitcast(BF16),
+                in_=x_rounded[:, h * HALF * PACK : (h + 1) * HALF * PACK],
             )
             x_codes.append(codes)
             x_scales.append(scales)

@@ -28,7 +28,7 @@ PSUM_BANKS = 8
 
 X_ORDER = (2, 0, 1, 3)
 W_LOADS = ((0, 56, 0), (56, 96, 40), (96, 128, 16))
-Y_VECTOR = 128
+Y_VECTOR = 176
 STORE_AFTER = {0: (0, 1), 1: (1, 2), 3: (2, 4)}
 
 
@@ -46,7 +46,6 @@ def tile_picked_tokscale_none_lo_kernel(tc, xT, tscale, cscale, w1, offs, out_0,
         nc.vector.memset(ts_window[0 : P - 1, :], 0.0)
         nc.scalar.dma_start(out=ts_window[P - 1 : P, :], in_=tscale[0:1, :])
 
-        nc.sync.dma_start(offsets[:], offs)
         x_planes = {}
         for j in X_ORDER:
             x_planes[j] = sb.tile([P, T], F32, name=f"x_plane_{j}", align_bytes=64)
@@ -54,6 +53,8 @@ def tile_picked_tokscale_none_lo_kernel(tc, xT, tscale, cscale, w1, offs, out_0,
             for i in range(pieces):
                 cols = slice(i * T // pieces, (i + 1) * T // pieces)
                 nc.sync.dma_start(out=x_planes[j][:, cols], in_=x_rows[:, j, cols])
+                if pieces == 2 and i == 0:
+                    nc.sync.dma_start(offsets[:], offs)
         w_raw = []
         for first, end, share in W_LOADS:
             raw = sb.tile([P, PACK, PACK * (end - first)], F32, name=f"w_raw_{first}", align_bytes=64)
@@ -171,11 +172,12 @@ def tile_picked_tokscale_none_lo_kernel(tc, xT, tscale, cscale, w1, offs, out_0,
                     lo, hi = STORE_AFTER[t]
                     nc.sync.dma_start(out=out_rows[:, lo:hi, cols], in_=y[h][:, lo:hi, :])
 
-        def round_y(h, share):
+        def round_y(h, share, first=0, end=HALF):
             dst = y_rounded[h][:].rearrange("p (c i t) -> p c t i", i=LINE, t=PACK)
             src = y[h][:].rearrange("p t (c i) -> p c t i", i=LINE)
-            for copy, lo, hi in shared(share // LINE, HALF // LINE):
-                copy(dst[:, lo:hi], src[:, lo:hi])
+            at = first // LINE
+            for copy, lo, hi in shared(share // LINE, (end - first) // LINE):
+                copy(dst[:, at + lo : at + hi], src[:, at + lo : at + hi])
 
         def quantize_y(first, end):
             h, at = divmod(first, HALF)
@@ -188,7 +190,8 @@ def tile_picked_tokscale_none_lo_kernel(tc, xT, tscale, cscale, w1, offs, out_0,
                 nc.sync.dma_start(out=out_words[:, end - HALF : end], in_=y_codes[h][:].bitcast(I32))
 
         product(0)
-        round_y(0, 0)
+        round_y(0, 0, 0, HALF // 2)
+        round_y(0, 0, HALF // 2, HALF)
         product(1)
         quantize_y(0, HALF // 2)
         round_y(1, Y_VECTOR)

@@ -26,8 +26,7 @@ QUADRANT = 32
 SCALE_ROWS = 4
 PSUM_BANKS = 8
 
-X_ORDER = (2, 0, 1, 3)
-W_LOADS = ((0, 56, 0), (56, 96, 40), (96, 128, 16))
+W_LOADS = ((0, 32, 0), (32, 64, 0), (64, 96, 24), (96, 128, 20))
 Y_VECTOR = 176
 STORE_AFTER = {0: (0, 1), 1: (1, 2), 3: (2, 4)}
 
@@ -46,15 +45,12 @@ def tile_picked_tokscale_none_lo_kernel(tc, xT, tscale, cscale, w1, offs, out_0,
         nc.vector.memset(ts_window[0 : P - 1, :], 0.0)
         nc.scalar.dma_start(out=ts_window[P - 1 : P, :], in_=tscale[0:1, :])
 
-        x_planes = {}
-        for j in X_ORDER:
-            x_planes[j] = sb.tile([P, T], F32, name=f"x_plane_{j}", align_bytes=64)
-            pieces = 2 if j == X_ORDER[0] else 1
-            for i in range(pieces):
-                cols = slice(i * T // pieces, (i + 1) * T // pieces)
-                nc.sync.dma_start(out=x_planes[j][:, cols], in_=x_rows[:, j, cols])
-                if pieces == 2 and i == 0:
-                    nc.sync.dma_start(offsets[:], offs)
+        nc.sync.dma_start(offsets[:], offs)
+        x_planes = []
+        for j in range(PACK):
+            plane = sb.tile([P, T], F32, name=f"x_plane_{j}", align_bytes=64)
+            nc.sync.dma_start(out=plane[:], in_=x_rows[:, j, :])
+            x_planes.append(plane)
         w_raw = []
         for first, end, share in W_LOADS:
             raw = sb.tile([P, PACK, PACK * (end - first)], F32, name=f"w_raw_{first}", align_bytes=64)
@@ -64,52 +60,49 @@ def tile_picked_tokscale_none_lo_kernel(tc, xT, tscale, cscale, w1, offs, out_0,
         nc.sync.dma_start(out=cs[:], in_=cscale.rearrange("(p t) o -> p (t o)", t=PACK))
 
         ones = sb.tile([P, P], F32)
-        ramp = sb.tile([P, P], F32, align_bytes=64)
+        ramp = sb.tile([P, P], F32, tag="x_rounded_0", align_bytes=64)
         ramp_turned = sb.tile([P, P], F32, align_bytes=64)
         ident = sb.tile([P, P], F32)
         nc.vector.memset(ones[:], 1.0)
         nc.vector.tensor_tensor_scan(ramp[:], ones[:], ones[:], 0.0, MULT, ADD)
         nc.vector.transpose(ramp_turned[:], ramp[:])
+        own = sb.tile([P, 1], F32)
         for q in range(0, P, QUADRANT):
             rows = slice(q, q + QUADRANT)
-            nc.vector.tensor_scalar(ident[rows, :], ramp[rows, :], ramp_turned[rows, q : q + 1], None, EQUAL)
+            nc.scalar.copy(own[rows, :], ramp_turned[rows, q : q + 1])
+        nc.vector.tensor_scalar(ident[:], ramp[:], own[:], None, EQUAL)
 
         def shared(share, width):
             parts = ((nc.vector.tensor_copy, 0, share), (nc.scalar.copy, share, width))
             return [(copy, lo, hi) for copy, lo, hi in parts if hi > lo]
 
-        tg_row = sb.tile([P, S], F32, align_bytes=64)
-        nc.vector.tensor_copy(tg_row[:], ts_window[:].indirect(offsets[:]))
-        turned = psum.tile([P, S // P, P], F32, tag="bank")
-        for b in range(S // P):
-            nc.tensor.transpose(turned[:, b, :], tg_row[:, b * P : (b + 1) * P], ident[:])
-
-        plane_2 = sb.tile([P, T], BF16, tag="plane_2", align_bytes=64)
-        for i in range(2):
-            cols = slice(i * T // 2, (i + 1) * T // 2)
-            nc.scalar.copy(plane_2[:, cols], x_planes[2][:, cols])
-
-        x_rounded = sb.tile([P, S * PACK], BF16, align_bytes=64)
-        x_slots = x_rounded[:].rearrange("p (s j) -> p s j", j=PACK)
-
         def entries(h):
             return offsets[:, h * HALF // LIST_ROWS : (h + 1) * HALF // LIST_ROWS]
 
-        nc.scalar.activation(x_slots[:, :, 2], plane_2[:].indirect(offsets[:]), COPY)
+        x_rounded = [sb.tile([P, HALF * PACK], BF16, name=f"x_rounded_{h}", align_bytes=64) for h in range(2)]
+        x_slots = [x_rounded[h][:].rearrange("p (s j) -> p s j", j=PACK) for h in range(2)]
+        picked = sb.tile([P, PACK, HALF], BF16, align_bytes=64)
 
-        picked = sb.tile([P, 2, S], F32, align_bytes=64)
-        nc.vector.tensor_copy(picked[:, 0, :], x_planes[0][:].indirect(offsets[:]))
-        tg_cols = sb.tile([P, S // P], F32, tag="plane_2", align_bytes=64)
-        nc.vector.tensor_copy(tg_cols[:], turned[:, :, P - 1])
+        def gather_plane(j):
+            nc.vector.tensor_copy(x_slots[0][:, :, j], x_planes[j][:].indirect(entries(0)))
+            nc.scalar.activation(picked[:, j, :], x_planes[j][:].indirect(entries(1)), COPY)
+
+        tg_row = sb.tile([P, S], F32, align_bytes=64)
+        nc.scalar.activation(tg_row[:], ts_window[:].indirect(offsets[:]), COPY)
+        turned = psum.tile([P, S // P, P], F32, tag="bank")
+        for b in range(S // P):
+            nc.tensor.transpose(turned[:, b, :], tg_row[:, b * P : (b + 1) * P], ident[:])
+        gather_plane(0)
+        gather_plane(1)
+        tg_cols = sb.tile([P, S // P], F32, tag="x_plane_1", align_bytes=64)
+        nc.scalar.copy(tg_cols[:], turned[:, :, P - 1])
         spread = psum.tile([P, S // P, P], F32, tag="bank")
         for b in range(S // P):
             nc.tensor.transpose(spread[:, b, :], tg_cols[:, b : b + 1].to_broadcast([P, P]), ident[:])
-        for h in range(2):
-            cols = slice(h * HALF, (h + 1) * HALF)
-            nc.vector.tensor_copy(picked[:, 1, cols], x_planes[1][:].indirect(entries(h)))
-            nc.scalar.copy(x_slots[:, cols, 0:2], picked[:, :, cols].rearrange("p j s -> p s j"))
-        for h in range(2):
-            nc.vector.tensor_copy(x_slots[:, h * HALF : (h + 1) * HALF, 3], x_planes[3][:].indirect(entries(h)))
+        gather_plane(2)
+        nc.vector.tensor_copy(x_slots[1][:, :, 0:3], picked[:, 0:3, :].rearrange("p j s -> p s j"))
+        gather_plane(3)
+        nc.vector.tensor_copy(x_slots[1][:, :, 3], picked[:, 3, :])
 
         x_codes, x_scales = [], []
 
@@ -119,7 +112,7 @@ def tile_picked_tokscale_none_lo_kernel(tc, xT, tscale, cscale, w1, offs, out_0,
             nc.vector.quantize_mx(
                 out=codes[:].bitcast(FP8X4),
                 scales=scales[:],
-                in_=x_rounded[:, h * HALF * PACK : (h + 1) * HALF * PACK],
+                in_=x_rounded[h][:],
             )
             x_codes.append(codes)
             x_scales.append(scales)

@@ -26,7 +26,8 @@ QUADRANT = 32
 SCALE_ROWS = 4
 PSUM_BANKS = 8
 
-W_LOADS = ((0, 32, 0), (32, 64, 0), (64, 96, 24), (96, 128, 20))
+X_VECTOR = (224, 256)
+W_LOADS = ((0, 32, 0), (32, 64, 0), (64, 96, 24), (96, 128, 16))
 Y_VECTOR = 176
 STORE_AFTER = {0: (0, 1), 1: (1, 2), 3: (2, 4)}
 
@@ -60,7 +61,7 @@ def tile_picked_tokscale_none_lo_kernel(tc, xT, tscale, cscale, w1, offs, out_0,
         nc.sync.dma_start(out=cs[:], in_=cscale.rearrange("(p t) o -> p (t o)", t=PACK))
 
         ones = sb.tile([P, P], F32)
-        ramp = sb.tile([P, P], F32, tag="x_rounded_0", align_bytes=64)
+        ramp = sb.tile([P, P], F32, tag="x_rounded", align_bytes=64)
         ramp_turned = sb.tile([P, P], F32, align_bytes=64)
         ident = sb.tile([P, P], F32)
         nc.vector.memset(ones[:], 1.0)
@@ -76,19 +77,22 @@ def tile_picked_tokscale_none_lo_kernel(tc, xT, tscale, cscale, w1, offs, out_0,
             parts = ((nc.vector.tensor_copy, 0, share), (nc.scalar.copy, share, width))
             return [(copy, lo, hi) for copy, lo, hi in parts if hi > lo]
 
-        def entries(h):
-            return offsets[:, h * HALF // LIST_ROWS : (h + 1) * HALF // LIST_ROWS]
-
-        x_rounded = [sb.tile([P, HALF * PACK], BF16, name=f"x_rounded_{h}", align_bytes=64) for h in range(2)]
-        x_slots = [x_rounded[h][:].rearrange("p (s j) -> p s j", j=PACK) for h in range(2)]
-        picked = sb.tile([P, PACK, HALF], BF16, align_bytes=64)
+        x_rounded = sb.tile([P, S * PACK], BF16, tag="x_rounded", align_bytes=64)
+        x_slots = x_rounded[:].rearrange("p (s j) -> p s j", j=PACK)
+        picked = [sb.tile([P, 2, S - split], BF16, name=f"picked_{split}", align_bytes=64) for split in X_VECTOR]
 
         def gather_plane(j):
-            nc.vector.tensor_copy(x_slots[0][:, :, j], x_planes[j][:].indirect(entries(0)))
-            nc.scalar.activation(picked[:, j, :], x_planes[j][:].indirect(entries(1)), COPY)
+            split = X_VECTOR[j // 2]
+            first, rest = offsets[:, : split // LIST_ROWS], offsets[:, split // LIST_ROWS :]
+            nc.vector.tensor_copy(x_slots[:, :split, j], x_planes[j][:].indirect(first))
+            nc.scalar.activation(picked[j // 2][:, j % 2, :], x_planes[j][:].indirect(rest), COPY)
+
+        def weave(j):
+            split = X_VECTOR[j // 2]
+            nc.vector.tensor_copy(x_slots[:, split:, j : j + 2], picked[j // 2][:].rearrange("p j s -> p s j"))
 
         tg_row = sb.tile([P, S], F32, align_bytes=64)
-        nc.scalar.activation(tg_row[:], ts_window[:].indirect(offsets[:]), COPY)
+        nc.vector.tensor_copy(tg_row[:], ts_window[:].indirect(offsets[:]))
         turned = psum.tile([P, S // P, P], F32, tag="bank")
         for b in range(S // P):
             nc.tensor.transpose(turned[:, b, :], tg_row[:, b * P : (b + 1) * P], ident[:])
@@ -99,10 +103,10 @@ def tile_picked_tokscale_none_lo_kernel(tc, xT, tscale, cscale, w1, offs, out_0,
         spread = psum.tile([P, S // P, P], F32, tag="bank")
         for b in range(S // P):
             nc.tensor.transpose(spread[:, b, :], tg_cols[:, b : b + 1].to_broadcast([P, P]), ident[:])
+        weave(0)
         gather_plane(2)
-        nc.vector.tensor_copy(x_slots[1][:, :, 0:3], picked[:, 0:3, :].rearrange("p j s -> p s j"))
         gather_plane(3)
-        nc.vector.tensor_copy(x_slots[1][:, :, 3], picked[:, 3, :])
+        weave(2)
 
         x_codes, x_scales = [], []
 
@@ -112,7 +116,7 @@ def tile_picked_tokscale_none_lo_kernel(tc, xT, tscale, cscale, w1, offs, out_0,
             nc.vector.quantize_mx(
                 out=codes[:].bitcast(FP8X4),
                 scales=scales[:],
-                in_=x_rounded[h][:],
+                in_=x_rounded[:, h * HALF * PACK : (h + 1) * HALF * PACK],
             )
             x_codes.append(codes)
             x_scales.append(scales)

@@ -27,7 +27,7 @@ SCALE_ROWS = 4
 PSUM_BANKS = 8
 
 X_VECTOR = (224, 256)
-W_LOADS = ((0, 32, 0), (32, 64, 0), (64, 96, 24), (96, 128, 16))
+W_LOADS = ((0, 56, 0), (56, 96, 40), (96, 128, 16))
 Y_VECTOR = 176
 STORE_AFTER = {0: (0, 1), 1: (1, 2), 3: (2, 4)}
 
@@ -46,11 +46,15 @@ def tile_picked_tokscale_none_lo_kernel(tc, xT, tscale, cscale, w1, offs, out_0,
         nc.vector.memset(ts_window[0 : P - 1, :], 0.0)
         nc.scalar.dma_start(out=ts_window[P - 1 : P, :], in_=tscale[0:1, :])
 
-        nc.sync.dma_start(offsets[:], offs)
         x_planes = []
         for j in range(PACK):
             plane = sb.tile([P, T], F32, name=f"x_plane_{j}", align_bytes=64)
-            nc.sync.dma_start(out=plane[:], in_=x_rows[:, j, :])
+            pieces = 2 if j == 0 else 1
+            for i in range(pieces):
+                cols = slice(i * T // pieces, (i + 1) * T // pieces)
+                nc.sync.dma_start(out=plane[:, cols], in_=x_rows[:, j, cols])
+                if pieces == 2 and i == 0:
+                    nc.sync.dma_start(offsets[:], offs)
             x_planes.append(plane)
         w_raw = []
         for first, end, share in W_LOADS:

@@ -20,16 +20,17 @@ COPY = mybir.ActivationFunctionType.Copy
 P = 128
 PACK = 4
 LINE = 4
-HALF = S // 2
 LIST_ROWS = 16
 QUADRANT = 32
 SCALE_ROWS = 4
 PSUM_BANKS = 8
 
-X_VECTOR = (224, 256)
-W_LOADS = ((0, 56, 0), (56, 96, 40), (96, 128, 16))
+CHUNKS = ((0, 128), (128, 256), (256, 512))
+X_VECTOR = (256, 128)
+TS_VECTOR = 256
+W_VECTOR = 84
 Y_VECTOR = 176
-STORE_AFTER = {0: (0, 1), 1: (1, 2), 3: (2, 4)}
+STORES = (((0, 2), (2, 4)), ((0, 2), (2, 4)), ((0, 2), (2, 4)))
 
 
 def tile_picked_tokscale_none_lo_kernel(tc, xT, tscale, cscale, w1, offs, out_0, out_1, out_2):
@@ -42,30 +43,24 @@ def tile_picked_tokscale_none_lo_kernel(tc, xT, tscale, cscale, w1, offs, out_0,
         w_rows = w1.rearrange("(p j) m -> p j m", j=PACK)
 
         offsets = sb.tile([P, S // LIST_ROWS], U16)
-        ts_window = sb.tile([P, T], F32, align_bytes=64)
+        ts_window = sb.tile([P, T], F32, align_bytes=256)
         nc.vector.memset(ts_window[0 : P - 1, :], 0.0)
         nc.scalar.dma_start(out=ts_window[P - 1 : P, :], in_=tscale[0:1, :])
 
+        w_raw = sb.tile([P, PACK, N], F32, align_bytes=256)
+        nc.sync.dma_start(out=w_raw[:, 0:2, :], in_=w_rows[:, 0:2, :])
+        nc.sync.dma_start(offsets[:], offs)
+        nc.sync.dma_start(out=w_raw[:, 2:4, :], in_=w_rows[:, 2:4, :])
         x_planes = []
         for j in range(PACK):
-            plane = sb.tile([P, T], F32, name=f"x_plane_{j}", align_bytes=64)
-            pieces = 2 if j == 0 else 1
-            for i in range(pieces):
-                cols = slice(i * T // pieces, (i + 1) * T // pieces)
-                nc.sync.dma_start(out=plane[:, cols], in_=x_rows[:, j, cols])
-                if pieces == 2 and i == 0:
-                    nc.sync.dma_start(offsets[:], offs)
+            plane = sb.tile([P, T], F32, name=f"x_plane_{j}", align_bytes=256)
+            nc.sync.dma_start(out=plane[:], in_=x_rows[:, j, :])
             x_planes.append(plane)
-        w_raw = []
-        for first, end, share in W_LOADS:
-            raw = sb.tile([P, PACK, PACK * (end - first)], F32, name=f"w_raw_{first}", align_bytes=64)
-            nc.sync.dma_start(out=raw[:], in_=w_rows[:, :, PACK * first : PACK * end])
-            w_raw.append(raw)
         cs = sb.tile([P, PACK], F32)
         nc.sync.dma_start(out=cs[:], in_=cscale.rearrange("(p t) o -> p (t o)", t=PACK))
 
         ones = sb.tile([P, P], F32)
-        ramp = sb.tile([P, P], F32, tag="x_rounded", align_bytes=64)
+        ramp = sb.tile([P, P], F32, align_bytes=64)
         ramp_turned = sb.tile([P, P], F32, align_bytes=64)
         ident = sb.tile([P, P], F32)
         nc.vector.memset(ones[:], 1.0)
@@ -77,127 +72,133 @@ def tile_picked_tokscale_none_lo_kernel(tc, xT, tscale, cscale, w1, offs, out_0,
             nc.scalar.copy(own[rows, :], ramp_turned[rows, q : q + 1])
         nc.vector.tensor_scalar(ident[:], ramp[:], own[:], None, EQUAL)
 
+        def entries(first, end):
+            return offsets[:, first // LIST_ROWS : end // LIST_ROWS]
+
         def shared(share, width):
             parts = ((nc.vector.tensor_copy, 0, share), (nc.scalar.copy, share, width))
             return [(copy, lo, hi) for copy, lo, hi in parts if hi > lo]
 
-        x_rounded = sb.tile([P, S * PACK], BF16, tag="x_rounded", align_bytes=64)
-        x_slots = x_rounded[:].rearrange("p (s j) -> p s j", j=PACK)
-        picked = [sb.tile([P, 2, S - split], BF16, name=f"picked_{split}", align_bytes=64) for split in X_VECTOR]
-
-        def gather_plane(j):
-            split = X_VECTOR[j // 2]
-            first, rest = offsets[:, : split // LIST_ROWS], offsets[:, split // LIST_ROWS :]
-            nc.vector.tensor_copy(x_slots[:, :split, j], x_planes[j][:].indirect(first))
-            nc.scalar.activation(picked[j // 2][:, j % 2, :], x_planes[j][:].indirect(rest), COPY)
-
-        def weave(j):
-            split = X_VECTOR[j // 2]
-            nc.vector.tensor_copy(x_slots[:, split:, j : j + 2], picked[j // 2][:].rearrange("p j s -> p s j"))
-
         tg_row = sb.tile([P, S], F32, align_bytes=64)
-        nc.vector.tensor_copy(tg_row[:], ts_window[:].indirect(offsets[:]))
+        nc.vector.tensor_copy(tg_row[:, :TS_VECTOR], ts_window[:].indirect(entries(0, TS_VECTOR)))
+        nc.scalar.activation(tg_row[:, TS_VECTOR:], ts_window[:].indirect(entries(TS_VECTOR, S)), COPY)
         turned = psum.tile([P, S // P, P], F32, tag="bank")
         for b in range(S // P):
             nc.tensor.transpose(turned[:, b, :], tg_row[:, b * P : (b + 1) * P], ident[:])
-        gather_plane(0)
-        gather_plane(1)
-        tg_cols = sb.tile([P, S // P], F32, tag="x_plane_1", align_bytes=64)
+        tg_cols = sb.tile([P, S // P], F32, align_bytes=64)
         nc.scalar.copy(tg_cols[:], turned[:, :, P - 1])
         spread = psum.tile([P, S // P, P], F32, tag="bank")
         for b in range(S // P):
             nc.tensor.transpose(spread[:, b, :], tg_cols[:, b : b + 1].to_broadcast([P, P]), ident[:])
-        weave(0)
-        gather_plane(2)
-        gather_plane(3)
-        weave(2)
 
-        x_codes, x_scales = [], []
+        w_dealt = sb.tile([P, PACK * P * PACK], BF16, align_bytes=256)
+        dst = w_dealt[:].rearrange("p (t m j) -> p m j t", t=PACK, j=PACK)
+        src = w_raw[:].rearrange("p j (m t) -> p m j t", t=PACK)
+        for copy, lo, hi in shared(W_VECTOR, P):
+            copy(dst[:, lo:hi], src[:, lo:hi])
+        w_codes = sb.tile([P, N], U32, align_bytes=256)
+        w_scales = sb.tile([P, N], U8, align_bytes=256)
+        nc.vector.quantize_mx(out=w_codes[:].bitcast(FP8X4), scales=w_scales[:], in_=w_dealt[:])
 
-        def quantize_x(h, tag):
-            codes = sb.tile([P, HALF], U32, name=f"x_codes_{h}", tag=tag, align_bytes=64)
-            scales = sb.tile([P, HALF], U8, name=f"x_scales_{h}", align_bytes=64)
-            nc.vector.quantize_mx(
-                out=codes[:].bitcast(FP8X4),
-                scales=scales[:],
-                in_=x_rounded[:, h * HALF * PACK : (h + 1) * HALF * PACK],
-            )
-            x_codes.append(codes)
-            x_scales.append(scales)
-
-        quantize_x(0, "x_codes_0")
-
-        w_dealt = sb.tile([P, PACK * P * PACK], BF16, tag="w_dealt", align_bytes=64)
-        for raw, (first, end, share) in zip(w_raw, W_LOADS):
-            dst = w_dealt[:].rearrange("p (t m j) -> p m j t", t=PACK, j=PACK)
-            src = raw[:].rearrange("p j (m t) -> p m j t", t=PACK)
-            for copy, lo, hi in shared(share, end - first):
-                copy(dst[:, first + lo : first + hi], src[:, lo:hi])
-
-        tg = sb.tile([P, S], F32, tag=f"w_raw_{W_LOADS[-1][0]}", align_bytes=64)
+        tg = sb.tile([P, S], F32, align_bytes=64)
         nc.scalar.copy(tg[:], spread[:].rearrange("p b n -> p (b n)"))
 
-        w_codes = [sb.tile([P, P], U32, name=f"w_codes_{t}", align_bytes=64) for t in range(PACK)]
-        w_scales = [sb.tile([P, P], U8, name=f"w_scales_{t}", align_bytes=64) for t in range(PACK)]
-        for t in range(PACK):
-            nc.vector.quantize_mx(
-                out=w_codes[t][:].bitcast(FP8X4),
-                scales=w_scales[t][:],
-                in_=w_dealt[:, t * P * PACK : (t + 1) * P * PACK],
+        x_rounded = sb.tile([P, S * PACK], BF16, align_bytes=256)
+        x_slots = x_rounded[:].rearrange("p (s j) -> p s j", j=PACK)
+        picked = [sb.tile([P, 2, S - split], BF16, name=f"picked_{split}", align_bytes=64) for split in X_VECTOR]
+
+        def gather_vector(j):
+            split = X_VECTOR[j // 2]
+            nc.vector.tensor_copy(x_slots[:, :split, j], x_planes[j][:].indirect(entries(0, split)))
+
+        def gather_scalar(j, first, end):
+            split = X_VECTOR[j // 2]
+            nc.scalar.activation(
+                picked[j // 2][:, j % 2, first - split : end - split], x_planes[j][:].indirect(entries(first, end)), COPY
             )
-        quantize_x(1, "w_dealt")
+
+        def weave(j, first, end):
+            split = X_VECTOR[j // 2]
+            pairs = picked[j // 2][:, :, first - split : end - split]
+            nc.vector.tensor_copy(x_slots[:, first:end, j : j + 2], pairs.rearrange("p j s -> p s j"))
+
+        x_codes = [sb.tile([P, end - first], U32, name=f"x_codes_{first}", align_bytes=256) for first, end in CHUNKS]
+        x_scales = [sb.tile([P, end - first], U8, name=f"x_scales_{first}", align_bytes=256) for first, end in CHUNKS]
+
+        def quantize_x(c):
+            first, end = CHUNKS[c]
+            nc.vector.quantize_mx(
+                out=x_codes[c][:].bitcast(FP8X4), scales=x_scales[c][:], in_=x_rounded[:, first * PACK : end * PACK]
+            )
+
+        for j in range(PACK - 1):
+            gather_vector(j)
+            gather_scalar(j, X_VECTOR[j // 2], S)
+            if j == 1:
+                weave(0, X_VECTOR[0], S)
+        gather_vector(3)
+        for first, end in CHUNKS[1:]:
+            gather_scalar(3, first, end)
+        weave(2, *CHUNKS[1])
+        quantize_x(0)
+        quantize_x(1)
+        weave(2, *CHUNKS[2])
 
         out_rows = out_0.rearrange("(p t) s -> p t s", t=PACK)
         out_words = out_1[0].rearrange("p s r -> p (s r)").bitcast(I32)
         out_scales = out_2[0].bitcast(I32)
         y_scales = sb.tile([P, S], U8, align_bytes=64)
-        y = [sb.tile([P, PACK, HALF], F32, name=f"y_{h}", align_bytes=64) for h in range(2)]
-        y_rounded = [sb.tile([P, HALF * PACK], BF16, name=f"y_rounded_{h}", align_bytes=64) for h in range(2)]
-        y_codes = [sb.tile([P, HALF], U32, name=f"y_codes_{h}", align_bytes=64) for h in range(2)]
+        y = [sb.tile([P, PACK, end - first], F32, name=f"y_{first}", align_bytes=64) for first, end in CHUNKS]
+        y_rounded = [sb.tile([P, (end - first) * PACK], BF16, name=f"y_rounded_{first}", align_bytes=64) for first, end in CHUNKS]
+        y_codes = [sb.tile([P, S // 2], U32, name=f"y_codes_{h}", align_bytes=64) for h in range(2)]
 
-        def product(h):
-            cols = slice(h * HALF, (h + 1) * HALF)
-            for t in range(PACK):
-                acc = psum.tile([P, HALF], F32, name=f"acc_{h}_{t}", tag="bank")
-                nc.tensor.matmul_mx(
-                    out=acc[:],
-                    lhsT=w_codes[t][:].bitcast(FP8X4),
-                    lhsT_scale=w_scales[t][:],
-                    rhs=x_codes[h][:].bitcast(FP8X4),
-                    rhs_scale=x_scales[h][:],
-                    start=True,
-                    stop=True,
-                )
-                nc.vector.scalar_tensor_tensor(y[h][:, t, :], acc[:], cs[:, t : t + 1], tg[:, cols], MULT, MULT)
-                if t in STORE_AFTER:
-                    lo, hi = STORE_AFTER[t]
-                    nc.sync.dma_start(out=out_rows[:, lo:hi, cols], in_=y[h][:, lo:hi, :])
-
-        def round_y(h, share, first=0, end=HALF):
-            dst = y_rounded[h][:].rearrange("p (c i t) -> p c t i", i=LINE, t=PACK)
-            src = y[h][:].rearrange("p t (c i) -> p c t i", i=LINE)
-            at = first // LINE
-            for copy, lo, hi in shared(share // LINE, (end - first) // LINE):
-                copy(dst[:, at + lo : at + hi], src[:, at + lo : at + hi])
-
-        def quantize_y(first, end):
-            h, at = divmod(first, HALF)
-            nc.vector.quantize_mx(
-                out=y_codes[h][:, at : at + end - first].bitcast(FP8X4),
-                scales=y_scales[:, first:end],
-                in_=y_rounded[h][:, PACK * at : PACK * (at + end - first)],
+        def product(c, t):
+            first, end = CHUNKS[c]
+            acc = psum.tile([P, end - first], F32, name=f"acc_{c}_{t}", tag="bank")
+            nc.tensor.matmul_mx(
+                out=acc[:],
+                lhsT=w_codes[:, t * P : (t + 1) * P].bitcast(FP8X4),
+                lhsT_scale=w_scales[:, t * P : (t + 1) * P],
+                rhs=x_codes[c][:].bitcast(FP8X4),
+                rhs_scale=x_scales[c][:],
+                start=True,
+                stop=True,
             )
-            if end % HALF == 0:
-                nc.sync.dma_start(out=out_words[:, end - HALF : end], in_=y_codes[h][:].bitcast(I32))
+            nc.vector.scalar_tensor_tensor(y[c][:, t, :], acc[:], cs[:, t : t + 1], tg[:, first:end], MULT, MULT)
+            for lo, hi in STORES[c]:
+                if hi == t + 1:
+                    nc.sync.dma_start(out=out_rows[:, lo:hi, first:end], in_=y[c][:, lo:hi, :])
 
-        product(0)
-        round_y(0, 0, 0, HALF // 2)
-        round_y(0, 0, HALF // 2, HALF)
-        product(1)
-        quantize_y(0, HALF // 2)
-        round_y(1, Y_VECTOR)
-        quantize_y(HALF // 2, HALF)
-        quantize_y(HALF, S)
+        def round_y(c, share):
+            first, end = CHUNKS[c]
+            dst = y_rounded[c][:].rearrange("p (c i t) -> p c t i", i=LINE, t=PACK)
+            src = y[c][:].rearrange("p t (c i) -> p c t i", i=LINE)
+            for copy, lo, hi in shared(share // LINE, (end - first) // LINE):
+                copy(dst[:, lo:hi], src[:, lo:hi])
+
+        def quantize_y(c):
+            first, end = CHUNKS[c]
+            h, at = divmod(first, S // 2)
+            nc.vector.quantize_mx(
+                out=y_codes[h][:, at : at + end - first].bitcast(FP8X4), scales=y_scales[:, first:end], in_=y_rounded[c][:]
+            )
+            if end % (S // 2) == 0:
+                nc.sync.dma_start(out=out_words[:, end - S // 2 : end], in_=y_codes[h][:].bitcast(I32))
+
+        product(0, 0)
+        quantize_x(2)
+        for t in range(1, PACK):
+            product(0, t)
+        round_y(0, 0)
+        for t in range(PACK):
+            product(1, t)
+        round_y(1, 0)
+        for t in range(PACK):
+            product(2, t)
+        quantize_y(0)
+        round_y(2, Y_VECTOR)
+        quantize_y(1)
+        quantize_y(2)
 
         for q in range(P // QUADRANT):
             queue = nc.scalar if q < 2 else nc.sync

@@ -26,6 +26,7 @@ SCALE_ROWS = 4
 PSUM_BANKS = 8
 
 CHUNKS = ((0, 128), (128, 256), (256, 512))
+QUARTER = 128
 X_VECTOR = (256, 128)
 TS_VECTOR = 256
 W_VECTOR = 84
@@ -117,19 +118,25 @@ def tile_picked_tokscale_none_lo_kernel(tc, xT, tscale, cscale, w1, offs, out_0,
                 picked[j // 2][:, j % 2, first - split : end - split], x_planes[j][:].indirect(entries(first, end)), COPY
             )
 
-        def weave(j, first, end):
+        def weave(j, first, end, copy=nc.vector.tensor_copy):
             split = X_VECTOR[j // 2]
             pairs = picked[j // 2][:, :, first - split : end - split]
-            nc.vector.tensor_copy(x_slots[:, first:end, j : j + 2], pairs.rearrange("p j s -> p s j"))
+            copy(x_slots[:, first:end, j : j + 2], pairs.rearrange("p j s -> p s j"))
 
-        x_codes = [sb.tile([P, end - first], U32, name=f"x_codes_{first}", align_bytes=256) for first, end in CHUNKS]
-        x_scales = [sb.tile([P, end - first], U8, name=f"x_scales_{first}", align_bytes=256) for first, end in CHUNKS]
+        x_codes, x_scales = [], []
 
-        def quantize_x(c):
-            first, end = CHUNKS[c]
+        def quarter(u):
+            return u * QUARTER, (u + 1) * QUARTER
+
+        def quantize_x(u, tag):
+            first, end = quarter(u)
+            codes = sb.tile([P, QUARTER], U32, name=f"x_codes_{u}", tag=tag, align_bytes=256)
+            scales = sb.tile([P, QUARTER], U8, name=f"x_scales_{u}", align_bytes=256)
             nc.vector.quantize_mx(
-                out=x_codes[c][:].bitcast(FP8X4), scales=x_scales[c][:], in_=x_rounded[:, first * PACK : end * PACK]
+                out=codes[:].bitcast(FP8X4), scales=scales[:], in_=x_rounded[:, first * PACK : end * PACK]
             )
+            x_codes.append(codes)
+            x_scales.append(scales)
 
         for j in range(PACK - 1):
             gather_vector(j)
@@ -137,12 +144,14 @@ def tile_picked_tokscale_none_lo_kernel(tc, xT, tscale, cscale, w1, offs, out_0,
             if j == 1:
                 weave(0, X_VECTOR[0], S)
         gather_vector(3)
-        for first, end in CHUNKS[1:]:
-            gather_scalar(3, first, end)
-        weave(2, *CHUNKS[1])
-        quantize_x(0)
-        quantize_x(1)
-        weave(2, *CHUNKS[2])
+        for u in range(1, PACK):
+            gather_scalar(3, *quarter(u))
+        weave(2, *quarter(1))
+        quantize_x(0, "x_codes_0")
+        weave(2, *quarter(2))
+        quantize_x(1, "x_codes_1")
+        weave(2, *quarter(3))
+        quantize_x(2, "x_codes_2")
 
         out_rows = out_0.rearrange("(p t) s -> p t s", t=PACK)
         out_words = out_1[0].rearrange("p s r -> p (s r)").bitcast(I32)
@@ -155,15 +164,16 @@ def tile_picked_tokscale_none_lo_kernel(tc, xT, tscale, cscale, w1, offs, out_0,
         def product(c, t):
             first, end = CHUNKS[c]
             acc = psum.tile([P, end - first], F32, name=f"acc_{c}_{t}", tag="bank")
-            nc.tensor.matmul_mx(
-                out=acc[:],
-                lhsT=w_codes[:, t * P : (t + 1) * P].bitcast(FP8X4),
-                lhsT_scale=w_scales[:, t * P : (t + 1) * P],
-                rhs=x_codes[c][:].bitcast(FP8X4),
-                rhs_scale=x_scales[c][:],
-                start=True,
-                stop=True,
-            )
+            for at in range(first, end, QUARTER):
+                nc.tensor.matmul_mx(
+                    out=acc[:, at - first : at - first + QUARTER],
+                    lhsT=w_codes[:, t * P : (t + 1) * P].bitcast(FP8X4),
+                    lhsT_scale=w_scales[:, t * P : (t + 1) * P],
+                    rhs=x_codes[at // QUARTER][:].bitcast(FP8X4),
+                    rhs_scale=x_scales[at // QUARTER][:],
+                    start=True,
+                    stop=True,
+                )
             nc.vector.scalar_tensor_tensor(y[c][:, t, :], acc[:], cs[:, t : t + 1], tg[:, first:end], MULT, MULT)
             for lo, hi in STORES[c]:
                 if hi == t + 1:
@@ -186,7 +196,7 @@ def tile_picked_tokscale_none_lo_kernel(tc, xT, tscale, cscale, w1, offs, out_0,
                 nc.sync.dma_start(out=out_words[:, end - S // 2 : end], in_=y_codes[h][:].bitcast(I32))
 
         product(0, 0)
-        quantize_x(2)
+        quantize_x(3, "x_codes_3")
         for t in range(1, PACK):
             product(0, t)
         round_y(0, 0)

@@ -30,7 +30,7 @@ QUARTER = 128
 X_VECTOR = (256, 128)
 TS_VECTOR = 256
 W_VECTOR = 84
-Y_VECTOR = 176
+Y_VECTOR = 136
 STORES = (((0, 2), (2, 4)), ((0, 2), (2, 4)), ((0, 2), (2, 4)))
 
 
@@ -196,8 +196,9 @@ def tile_picked_tokscale_none_lo_kernel(tc, xT, tscale, cscale, w1, offs, out_0,
                 nc.sync.dma_start(out=out_words[:, end - S // 2 : end], in_=y_codes[h][:].bitcast(I32))
 
         product(0, 0)
+        product(0, 1)
         quantize_x(3, "x_codes_3")
-        for t in range(1, PACK):
+        for t in range(2, PACK):
             product(0, t)
         round_y(0, 0)
         for t in range(PACK):

@@ -156,10 +156,10 @@ def tile_picked_tokscale_none_lo_kernel(tc, xT, tscale, cscale, w1, offs, out_0,
         out_rows = out_0.rearrange("(p t) s -> p t s", t=PACK)
         out_words = out_1[0].rearrange("p s r -> p (s r)").bitcast(I32)
         out_scales = out_2[0].bitcast(I32)
-        y_scales = sb.tile([P, S], U8, align_bytes=64)
-        y = [sb.tile([P, PACK, end - first], F32, name=f"y_{first}", align_bytes=64) for first, end in CHUNKS]
+        y_scales = sb.tile([P, S], U8, align_bytes=256)
+        y = [sb.tile([P, PACK, end - first], F32, name=f"y_{first}", align_bytes=256) for first, end in CHUNKS]
         y_rounded = [sb.tile([P, (end - first) * PACK], BF16, name=f"y_rounded_{first}", align_bytes=64) for first, end in CHUNKS]
-        y_codes = [sb.tile([P, S // 2], U32, name=f"y_codes_{h}", align_bytes=64) for h in range(2)]
+        y_codes = [sb.tile([P, S // 2], U32, name=f"y_codes_{h}", align_bytes=256) for h in range(2)]
 
         def product(c, t):
             first, end = CHUNKS[c]

from contextlib import ExitStack

import concourse.mybir as mybir

K, T, S, N = 512, 1024, 512, 512
FLOPS = 2 * K * S * N

F32 = mybir.dt.float32
BF16 = mybir.dt.bfloat16
I32 = mybir.dt.int32
U32 = mybir.dt.uint32
U16 = mybir.dt.uint16
U8 = mybir.dt.uint8
FP8X4 = mybir.dt.float8_e4m3fn_x4
MULT = mybir.AluOpType.mult
ADD = mybir.AluOpType.add
EQUAL = mybir.AluOpType.is_equal
COPY = mybir.ActivationFunctionType.Copy

P = 128
PACK = 4
LINE = 4
LIST_ROWS = 16
QUADRANT = 32
SCALE_ROWS = 4
PSUM_BANKS = 8

CHUNKS = ((0, 128), (128, 256), (256, 512))
QUARTER = 128
X_VECTOR = (256, 128)
TS_VECTOR = 256
W_VECTOR = 84
Y_VECTOR = 136
STORES = (((0, 2), (2, 4)), ((0, 2), (2, 4)), ((0, 2), (2, 4)))


def tile_picked_tokscale_none_lo_kernel(tc, xT, tscale, cscale, w1, offs, out_0, out_1, out_2):
    nc = tc.nc
    with ExitStack() as ctx:
        sb = ctx.enter_context(tc.tile_pool(name="sb", bufs=1))
        psum = ctx.enter_context(tc.psum_pool(name="psum", bufs=PSUM_BANKS))

        x_rows = xT.rearrange("(p j) t -> p j t", j=PACK)
        w_rows = w1.rearrange("(p j) m -> p j m", j=PACK)

        offsets = sb.tile([P, S // LIST_ROWS], U16)
        ts_window = sb.tile([P, T], F32, align_bytes=256)
        nc.vector.memset(ts_window[0 : P - 1, :], 0.0)
        nc.scalar.dma_start(out=ts_window[P - 1 : P, :], in_=tscale[0:1, :])

        w_raw = sb.tile([P, PACK, N], F32, align_bytes=256)
        nc.sync.dma_start(out=w_raw[:, 0:2, :], in_=w_rows[:, 0:2, :])
        nc.sync.dma_start(offsets[:], offs)
        nc.sync.dma_start(out=w_raw[:, 2:4, :], in_=w_rows[:, 2:4, :])
        x_planes = []
        for j in range(PACK):
            plane = sb.tile([P, T], F32, name=f"x_plane_{j}", align_bytes=256)
            nc.sync.dma_start(out=plane[:], in_=x_rows[:, j, :])
            x_planes.append(plane)
        cs = sb.tile([P, PACK], F32)
        nc.sync.dma_start(out=cs[:], in_=cscale.rearrange("(p t) o -> p (t o)", t=PACK))

        ones = sb.tile([P, P], F32)
        ramp = sb.tile([P, P], F32, align_bytes=64)
        ramp_turned = sb.tile([P, P], F32, align_bytes=64)
        ident = sb.tile([P, P], F32)
        nc.vector.memset(ones[:], 1.0)
        nc.vector.tensor_tensor_scan(ramp[:], ones[:], ones[:], 0.0, MULT, ADD)
        nc.vector.transpose(ramp_turned[:], ramp[:])
        own = sb.tile([P, 1], F32)
        for q in range(0, P, QUADRANT):
            rows = slice(q, q + QUADRANT)
            nc.scalar.copy(own[rows, :], ramp_turned[rows, q : q + 1])
        nc.vector.tensor_scalar(ident[:], ramp[:], own[:], None, EQUAL)

        def entries(first, end):
            return offsets[:, first // LIST_ROWS : end // LIST_ROWS]

        def shared(share, width):
            parts = ((nc.vector.tensor_copy, 0, share), (nc.scalar.copy, share, width))
            return [(copy, lo, hi) for copy, lo, hi in parts if hi > lo]

        tg_row = sb.tile([P, S], F32, align_bytes=64)
        nc.vector.tensor_copy(tg_row[:, :TS_VECTOR], ts_window[:].indirect(entries(0, TS_VECTOR)))
        nc.scalar.activation(tg_row[:, TS_VECTOR:], ts_window[:].indirect(entries(TS_VECTOR, S)), COPY)
        turned = psum.tile([P, S // P, P], F32, tag="bank")
        for b in range(S // P):
            nc.tensor.transpose(turned[:, b, :], tg_row[:, b * P : (b + 1) * P], ident[:])
        tg_cols = sb.tile([P, S // P], F32, align_bytes=64)
        nc.scalar.copy(tg_cols[:], turned[:, :, P - 1])
        spread = psum.tile([P, S // P, P], F32, tag="bank")
        for b in range(S // P):
            nc.tensor.transpose(spread[:, b, :], tg_cols[:, b : b + 1].to_broadcast([P, P]), ident[:])

        w_dealt = sb.tile([P, PACK * P * PACK], BF16, align_bytes=256)
        dst = w_dealt[:].rearrange("p (t m j) -> p m j t", t=PACK, j=PACK)
        src = w_raw[:].rearrange("p j (m t) -> p m j t", t=PACK)
        for copy, lo, hi in shared(W_VECTOR, P):
            copy(dst[:, lo:hi], src[:, lo:hi])
        w_codes = sb.tile([P, N], U32, align_bytes=256)
        w_scales = sb.tile([P, N], U8, align_bytes=256)
        nc.vector.quantize_mx(out=w_codes[:].bitcast(FP8X4), scales=w_scales[:], in_=w_dealt[:])

        tg = sb.tile([P, S], F32, align_bytes=64)
        nc.scalar.copy(tg[:], spread[:].rearrange("p b n -> p (b n)"))

        x_rounded = sb.tile([P, S * PACK], BF16, align_bytes=256)
        x_slots = x_rounded[:].rearrange("p (s j) -> p s j", j=PACK)
        picked = [sb.tile([P, 2, S - split], BF16, name=f"picked_{split}", align_bytes=64) for split in X_VECTOR]

        def gather_vector(j):
            split = X_VECTOR[j // 2]
            nc.vector.tensor_copy(x_slots[:, :split, j], x_planes[j][:].indirect(entries(0, split)))

        def gather_scalar(j, first, end):
            split = X_VECTOR[j // 2]
            nc.scalar.activation(
                picked[j // 2][:, j % 2, first - split : end - split], x_planes[j][:].indirect(entries(first, end)), COPY
            )

        def weave(j, first, end, copy=nc.vector.tensor_copy):
            split = X_VECTOR[j // 2]
            pairs = picked[j // 2][:, :, first - split : end - split]
            copy(x_slots[:, first:end, j : j + 2], pairs.rearrange("p j s -> p s j"))

        x_codes, x_scales = [], []

        def quarter(u):
            return u * QUARTER, (u + 1) * QUARTER

        def quantize_x(u, tag):
            first, end = quarter(u)
            codes = sb.tile([P, QUARTER], U32, name=f"x_codes_{u}", tag=tag, align_bytes=256)
            scales = sb.tile([P, QUARTER], U8, name=f"x_scales_{u}", align_bytes=256)
            nc.vector.quantize_mx(
                out=codes[:].bitcast(FP8X4), scales=scales[:], in_=x_rounded[:, first * PACK : end * PACK]
            )
            x_codes.append(codes)
            x_scales.append(scales)

        for j in range(PACK - 1):
            gather_vector(j)
            gather_scalar(j, X_VECTOR[j // 2], S)
            if j == 1:
                weave(0, X_VECTOR[0], S)
        gather_vector(3)
        for u in range(1, PACK):
            gather_scalar(3, *quarter(u))
        weave(2, *quarter(1))
        quantize_x(0, "x_codes_0")
        weave(2, *quarter(2))
        quantize_x(1, "x_codes_1")
        weave(2, *quarter(3))
        quantize_x(2, "x_codes_2")

        out_rows = out_0.rearrange("(p t) s -> p t s", t=PACK)
        out_words = out_1[0].rearrange("p s r -> p (s r)").bitcast(I32)
        out_scales = out_2[0].bitcast(I32)
        y_scales = sb.tile([P, S], U8, align_bytes=256)
        y = [sb.tile([P, PACK, end - first], F32, name=f"y_{first}", align_bytes=256) for first, end in CHUNKS]
        y_rounded = [sb.tile([P, (end - first) * PACK], BF16, name=f"y_rounded_{first}", align_bytes=64) for first, end in CHUNKS]
        y_codes = [sb.tile([P, S // 2], U32, name=f"y_codes_{h}", align_bytes=256) for h in range(2)]

        def product(c, t):
            first, end = CHUNKS[c]
            acc = psum.tile([P, end - first], F32, name=f"acc_{c}_{t}", tag="bank")
            for at in range(first, end, QUARTER):
                nc.tensor.matmul_mx(
                    out=acc[:, at - first : at - first + QUARTER],
                    lhsT=w_codes[:, t * P : (t + 1) * P].bitcast(FP8X4),
                    lhsT_scale=w_scales[:, t * P : (t + 1) * P],
                    rhs=x_codes[at // QUARTER][:].bitcast(FP8X4),
                    rhs_scale=x_scales[at // QUARTER][:],
                    start=True,
                    stop=True,
                )
            nc.vector.scalar_tensor_tensor(y[c][:, t, :], acc[:], cs[:, t : t + 1], tg[:, first:end], MULT, MULT)
            for lo, hi in STORES[c]:
                if hi == t + 1:
                    nc.sync.dma_start(out=out_rows[:, lo:hi, first:end], in_=y[c][:, lo:hi, :])

        def round_y(c, share):
            first, end = CHUNKS[c]
            dst = y_rounded[c][:].rearrange("p (c i t) -> p c t i", i=LINE, t=PACK)
            src = y[c][:].rearrange("p t (c i) -> p c t i", i=LINE)
            for copy, lo, hi in shared(share // LINE, (end - first) // LINE):
                copy(dst[:, lo:hi], src[:, lo:hi])

        def quantize_y(c):
            first, end = CHUNKS[c]
            h, at = divmod(first, S // 2)
            nc.vector.quantize_mx(
                out=y_codes[h][:, at : at + end - first].bitcast(FP8X4), scales=y_scales[:, first:end], in_=y_rounded[c][:]
            )
            if end % (S // 2) == 0:
                nc.sync.dma_start(out=out_words[:, end - S // 2 : end], in_=y_codes[h][:].bitcast(I32))

        product(0, 0)
        product(0, 1)
        quantize_x(3, "x_codes_3")
        for t in range(2, PACK):
            product(0, t)
        round_y(0, 0)
        for t in range(PACK):
            product(1, t)
        round_y(1, 0)
        for t in range(PACK):
            product(2, t)
        quantize_y(0)
        round_y(2, Y_VECTOR)
        quantize_y(1)
        quantize_y(2)

        for q in range(P // QUADRANT):
            queue = nc.scalar if q < 2 else nc.sync
            queue.dma_start(
                out=out_scales[SCALE_ROWS * q : SCALE_ROWS * (q + 1), :],
                in_=y_scales[:].bitcast(I32)[QUADRANT * q : QUADRANT * q + SCALE_ROWS, :],
            )
